import numpy as np, ml_dtypes
CORES = [35,38,43,46]
N = 4
BF = ml_dtypes.bfloat16
def gentries(a):
    return np.ascontiguousarray(a.reshape(8, 16, -1).transpose(0, 2, 1)).reshape(8, -1)
def gtable(e):
    e = np.asarray(e); return np.ascontiguousarray(e.reshape(8, -1, 16).transpose(0, 2, 1)).reshape(128, -1).astype(np.int32)
L, XW, YW, R, SL = 2, 64, 64, 1024, 48
C = XW * YW
SLR = np.arange(128) % 16 >= 14
def pack(e, fc, x, v, u, w):
    g = lambda a: np.stack([gtable(t) for t in a])
    return {"lay": e.astype(np.float32).astype(BF), "fac": np.repeat(fc, 16, axis=1).astype(np.int32), "px": g(x), "py": g(v), "dx": g(u), "dy": g(w)}
def parts(rng):
    e = rng.integers(-120, 121, (N, 128, L * C), dtype=np.int16)
    e[:, SLR] = rng.integers(-SL, SL + 1, (N, 16, L * C), dtype=np.int16)
    fc = np.stack([np.stack([rng.permutation(16)[:8] + 1 for l in range(L)], axis=1) for r in range(N)])
    return [e, fc, rng.integers(0, 16 * XW, (N, 8, R)), rng.integers(0, 16 * YW, (N, 8, R)), rng.integers(-16, 17, (N, 8, R)), rng.integers(-16, 17, (N, 8, R))]
def setup_inputs(rng):
    return pack(*parts(rng))
def setup_inputs_prism(rng):
    e, fc, x, v, u, w = parts(rng)
    return pack(np.tile(e[:, :16], (1, 8, 1)), fc, *[np.repeat(a[:, :1], 8, axis=1) for a in (x, v, u, w)])
def setup_inputs_steep(rng):
    e, fc, x, v, u, w = parts(rng); g = int(rng.integers(0, 8))
    e[:, SLR] = SL * rng.choice(np.array([-1, 1]), (N, 16, L * C)); fc[:] = 16
    u = 16 * rng.choice(np.array([-1, 1]), u.shape); w = 16 * rng.choice(np.array([-1, 1]), w.shape)
    e[:, 16 * g] = 120; e[:, 16 * g + 1] = -120; e[:, 16 * g + 14] = SL; e[:, 16 * g + 15] = -SL; u[:, g] = 16; w[:, g] = -16
    return pack(e, fc, x, v, u, w)
def setup_inputs_edges(rng):
    e, fc, x, v, u, w = parts(rng)
    e[:, SLR] = rng.choice(np.array([-8, -1, 0, 1, 8]), (N, 16, L * C)); fc = rng.choice(np.array([1, 2, 15, 16]), fc.shape)
    x = rng.choice(np.array([0, 15, 16, 16 * XW - 16, 16 * XW - 1]), x.shape); v = rng.choice(np.array([0, 15, 16, 16 * YW - 16, 16 * YW - 1]), v.shape)
    u = rng.choice(np.array([-16, -1, 0, 1, 16]), u.shape); w = rng.choice(np.array([-16, -1, 0, 1, 16]), w.shape)
    return pack(e, fc, x, v, u, w)
def setup_inputs_one(rng):
    p = parts(rng); q = int(rng.integers(0, N))
    for i in range(2, 6):
        p[i] = np.repeat(p[i][:, :, :16], R // 16, axis=2); p[i][q] = p[i][q][:, :1]
    return pack(*p)
def setup_inputs_spread(rng):
    e, fc, x, v, u, w = parts(rng)
    z = rng.random(e.shape, dtype=np.float32); e[z < 0.5] = 0; k = z > 0.9; b = np.where(SLR, SL, 120)[None, :, None]
    e = np.where(k, np.where(e < 0, -b, b), e)
    x = np.floor(rng.random(x.shape) ** 4 * (16 * XW)).astype(np.int64); v = np.floor(rng.random(v.shape) ** 4 * (16 * YW)).astype(np.int64)
    return pack(e, fc, x, v, u, w)
def check_inputs(d):
    bad = []; e = d["lay"].astype(np.float32); fc = d["fac"]
    if not np.array_equal(e, np.floor(e)): bad.append("whole numbers in lay")
    if not np.abs(e[:, ~SLR]).max() <= 120: bad.append("emission")
    if not np.abs(e[:, SLR]).max() <= SL: bad.append("slopes")
    if not (fc.min() >= 1 and fc.max() <= 16): bad.append("factors")
    if not np.array_equal(fc, np.repeat(fc[:, ::16], 16, axis=1)): bad.append("factors alike in a group")
    if not (d["px"].min() >= 0 and d["px"].max() < 16 * XW and d["py"].min() >= 0 and d["py"].max() < 16 * YW): bad.append("places")
    if not (min(d["dx"].min(), d["dy"].min()) >= -16 and max(d["dx"].max(), d["dy"].max()) <= 16): bad.append("directions")
    return bad
def reference(lay, fac, px, py, dx, dy):
    t = lay.astype(np.float32).astype(np.int32).reshape(N, 8, 16, L, C)
    y = np.zeros((N, 128, R), np.float32); g8 = np.arange(8)[:, None, None]; c16 = np.arange(16)[None, :, None]
    for r in range(N):
        x, v, u, w = [gentries(a[r]).astype(np.int64) for a in (px, py, dx, dy)]
        s = np.zeros((8, 16, R), np.int64)
        for h in range(N):
            q = (r + h) % N
            for l in range(L):
                fc = fac[q, ::16, l].astype(np.int64)[:, None]
                cell = (v >> 4) * XW + (x >> 4)
                p = t[q][g8, c16, l, cell[:, None, :]].astype(np.int64)
                s = s + p
                u = u + ((fc * p[:, 14]) >> 7); w = w + ((fc * p[:, 15]) >> 7)
                x = (x + u) & (16 * XW - 1); v = (v + w) & (16 * YW - 1)
        y[r] = s.reshape(128, R).astype(np.float32)
    return {"y": y}

@@ -1,0 +1,343 @@
+from concourse.bass import DstId, RemoteDMATransfer
+from concourse.mybir import AluOpType, ActivationFunctionType
+
+C = 4096
+R = 1024
+K = R // 16
+BW = 144
+PIECES = [(0, 1344), (1344, 2720), (2720, C)]
+ROUND = 12582912.0
+KAPPA = -127.0 / 256.0
+SHIFT = 512
+
+SCRATCH = {
+    "w0": ("sbuf", [128, C], "bfloat16"),
+    "w1": ("sbuf", [128, C], "bfloat16"),
+    "v0": ("sbuf", [128, C], "bfloat16"),
+    "v1": ("sbuf", [128, C], "bfloat16"),
+    "p": ("sbuf", [128, 8 * R], "bfloat16"),
+    "pxy": ("sbuf", [128, 2 * K], "int32"),
+    "dxy": ("sbuf", [128, 2 * K], "int32"),
+    "fo": ("sbuf", [128, 8], "int32"),
+    "fp0": ("sbuf", [128, 8], "int32"),
+    "fp1": ("sbuf", [128, 8], "int32"),
+    "ff": ("sbuf", [128, 8], "float32"),
+    "pi": ("sbuf", [128, 8], "int32"),
+    "pm": ("sbuf", [128, 8], "int32"),
+    "mk": ("sbuf", [128, 8], "float32"),
+    "dg": ("sbuf", [128, BW], "float32"),
+    "dm": ("sbuf", [128, 2 * BW], "bfloat16"),
+    "band": ("sbuf", [128, 8 * BW], "bfloat16"),
+    "ib": ("sbuf", [128, 128], "bfloat16"),
+    "ih": ("sbuf", [128, 128], "float16"),
+    "i2": ("sbuf", [128, 128], "float16"),
+    "im": ("sbuf", [128, 128], "float16"),
+    "kap": ("sbuf", [128, K], "bfloat16"),
+    "pos": ("sbuf", [128, 10 * 2 * K], "float16"),
+    "z": ("sbuf", [128, 2 * K], "int32"),
+    "cc": ("sbuf", [128, 2 * K], "int32"),
+    "cs": ("sbuf", [128, K], "int32"),
+    "t0": ("sbuf", [128, 2 * K], "int32"),
+    "off": ("sbuf", [128, 8 * K], "uint16"),
+    "mo0": ("sbuf", [128, 5 * K], "uint16"),
+    "mo1": ("sbuf", [128, 5 * K], "uint16"),
+    "mi0": ("sbuf", [128, 5 * K], "uint16"),
+    "mi1": ("sbuf", [128, 5 * K], "uint16"),
+    "po": ("sbuf", [128, R], "float16"),
+    "pin": ("sbuf", [128, R], "float16"),
+    "yo": ("sbuf", [128, R], "float32"),
+    "psx": ("psum", [128, 512], "float32"),
+    "psy": ("psum", [128, 512], "float32"),
+    "aoa": ("psum", [128, 512], "float32"),
+    "aob": ("psum", [128, 512], "float32"),
+    "apa": ("psum", [128, 512], "float32"),
+    "apb": ("psum", [128, 512], "float32"),
+}
+SEMAPHORES = [
+    "lp", "ld", "lf", "lw0", "lw1a", "lw1b", "lw1c", "gi", "su", "dv", "dx", "ga", "gd", "mx", "my", "ep", "cv",
+    "ac", "eva", "evb", "fa", "fb", "ya", "yb", "sa", "sb", "sent",
+    "af", "av0", "av1", "am0", "am1", "apa_in", "apb_in", "hf", "h0", "h1", "h2",
+]
+
+
+def bits(m):
+    return bin(m).count("1")
+
+
+def relay_core(src, dst, cores, topo):
+    for h in topo.cores_of(src):
+        if h not in cores and topo.die(h) != topo.die(src) and topo.may_write(h, dst):
+            return h
+    return None
+
+
+def routes(T, topo):
+    cores = list(T.cores)
+    n = len(cores)
+    out = []
+    for r in range(n):
+        s, d, partner = cores[r], cores[(r + 1) % n], cores[(r + 2) % n]
+        near = [c for c in topo.cores_of(s) if c != s][0]
+        lo = topo.mask(s, partner)
+        hi = topo.mask(s, near) & ~lo
+        h = None if topo.chip(s) == topo.chip(d) else relay_core(s, d, cores, topo)
+        out.append((s, d, h, lo, hi))
+    return out
+
+
+def send(g, topo, dst, out_ap, in_ap, rsem, lsem, mask):
+    rid, pid, _se = topo.addr(dst)
+    g.remote_dma(out_ap, in_ap, rsem, lsem, pid, rid, mask)
+
+
+def relay_program(g, core, d, hi, T, topo):
+    S = T.sem
+    m = topo.mask(core, d)
+    g.wait_ge(S.hf, bits(hi))
+    send(g, topo, d, T.fp1[:, 0:1], T.fp1[:, 0:1], S.af, S.sent, m)
+    for k, (a, b) in enumerate(PIECES):
+        g.wait_ge(S["h%d" % k], bits(hi))
+        send(g, topo, d, T.v1[:, a:b], T.v1[:, a:b], S.av1, S.sent, m)
+    g.wait_ge(S.sent, bits(m) * (1 + len(PIECES)))
+
+
+def rank_program(g, core, T, topo):
+    rank = T.rank_of(core)
+    rts = routes(T, topo)
+    if rank is None:
+        for (s, d, h, lo, hi) in rts:
+            if h == core:
+                relay_program(g, core, d, hi, T, topo)
+        return
+    n = len(rts)
+    S = T.sem
+    V, A, PE, SY = g.vector, g.scalar, g.tensor, g.sync
+    op = AluOpType
+    _s, nxt, helper, lo, hi = rts[rank]
+    prev, _me, phelper, plo, phi = rts[(rank - 1) % n]
+    partner = rts[(rank + 2) % n][0]
+    cnt = {}
+
+    def inc(ins, name, k=1):
+        ins.then_inc(S[name], k)
+        cnt[name] = cnt.get(name, 0) + k
+
+    def wait(q, name):
+        q.wait_ge(S[name], cnt[name])
+
+    hop_in = bits(topo.mask(partner, core))
+    if phelper is None:
+        cnt["af"] = bits(plo) + bits(phi)
+        cnt["av0"] = bits(plo | phi)
+        cnt["av1"] = bits(phi)
+    else:
+        cnt["af"] = bits(plo) + bits(topo.mask(phelper, core))
+        cnt["av0"] = bits(plo)
+        cnt["av1"] = bits(topo.mask(phelper, core)) * len(PIECES)
+    for nm in ("am0", "am1", "apa_in", "apb_in"):
+        cnt[nm] = hop_in
+    cnt["sent"] = 0
+
+    inc(A.dma_start(T.fo[:, 0:2], T.fac[:]), "lf", 16)
+    inc(SY.dma_start(T.pxy[:, 0:K], T.px[:]), "lp", 16)
+    inc(A.dma_start(T.pxy[:, K:2 * K], T.py[:]), "lp", 16)
+    inc(SY.dma_start(T.dxy[:, 0:K], T.dx[:]), "ld", 16)
+    inc(A.dma_start(T.dxy[:, K:2 * K], T.dy[:]), "ld", 16)
+    inc(SY.dma_start(T.w0[:], T.lay[:, 0:C]), "lw0", 16)
+    w1_pieces = PIECES if helper is not None else [(0, C)]
+    w1_sems = ["lw1a", "lw1b", "lw1c"][:len(w1_pieces)]
+    for (a, b), nm in zip(w1_pieces, w1_sems):
+        inc(SY.dma_start(T.w1[:, a:b], T.lay[:, C + a:C + b]), nm, 16)
+
+    inc(g.iota(T.dg[:], [[1, BW]], -1, -1, allow_small_or_imprecise_dtypes=True), "gi")
+    inc(g.iota(T.pi[:, 0:1], [[1, 1]], 0, 1), "gi")
+    inc(V.memset(T.kap[:], KAPPA), "su")
+    wait(V, "gi")
+    inc(V.tensor_scalar(T.pm[:, 0:1], T.pi[:, 0:1], 15, None, op.bitwise_and), "su")
+    for buf, val in ((T.ib, 1.0), (T.ih, 1.0), (T.i2, 2.0), (T.im, -1.0)):
+        inc(V.tensor_scalar(buf[:], T.dg[:, 0:128], -1.0, val, op.is_equal, op.mult), "su")
+    wait(V, "su")
+    for a in range(2):
+        inc(V.tensor_scalar(T.mk[:, a:a + 1], T.pm[:, 0:1], float(14 + a), 1.0 / 128, op.is_equal, op.mult), "su")
+    wait(V, "su")
+    for a in range(2):
+        inc(V.tensor_scalar(T.dm[:, a * BW:(a + 1) * BW], T.dg[:], 0.0, T.mk[:, a:a + 1], op.is_equal, op.mult), "su")
+
+    def dst_of(c):
+        rid, pid, _se = topo.addr(c)
+        return DstId(rid=rid, pnc=pid)
+
+    second = nxt if helper is None else helper
+    wait(g, "lf")
+    g.remote_dma_fused([
+        RemoteDMATransfer(dst_ids=[dst_of(nxt)], dma_engine_mask=lo, remote_sem=S.af,
+                          src=T.fo[:, 0:1], dst=T.fp0[:, 0:1]),
+        RemoteDMATransfer(dst_ids=[dst_of(second)], dma_engine_mask=hi,
+                          remote_sem=S.af if helper is None else S.hf, src=T.fo[:, 1:2], dst=T.fp1[:, 0:1]),
+    ], local_sem=S.sent)
+    cnt["sent"] += bits(lo) + bits(hi)
+    wait(g, "lw0")
+    m0 = (lo | hi) if helper is None else lo
+    send(g, topo, nxt, T.v0[:], T.w0[:], S.av0, S.sent, m0)
+    cnt["sent"] += bits(m0)
+    for k, ((a, b), nm) in enumerate(zip(w1_pieces, w1_sems)):
+        wait(g, nm)
+        send(g, topo, second, T.v1[:, a:b], T.w1[:, a:b], S.av1 if helper is None else S["h%d" % k], S.sent, hi)
+        cnt["sent"] += bits(hi)
+
+    def slot(k, a=None):
+        if a is None:
+            return T.pos[:, 2 * K * k:2 * K * (k + 1)]
+        return T.pos[:, 2 * K * k + K * a:2 * K * k + K * (a + 1)]
+
+    wait(V, "lp")
+    inc(V.tensor_scalar(T.cc[:], T.pxy[:], 4, None, op.arith_shift_right), "dv")
+    inc(V.tensor_scalar(slot(1), T.pxy[:], float(SHIFT), None, op.add), "su")
+    wait(V, "dv")
+    inc(V.tensor_scalar(T.z[:, K:2 * K], T.cc[:, K:2 * K], 64.0, None, op.mult), "dv")
+    wait(V, "dv")
+    inc(V.tensor_tensor(T.cs[:], T.cc[:, 0:K], T.z[:, K:2 * K], op.add), "dv")
+    wait(V, "dv")
+    inc(V.tensor_copy(T.off[:, 0:K], T.cs[:]), "dv")
+    wait(V, "lf")
+    wait(V, "ld")
+    inc(V.tensor_copy(T.ff[:, 0:2], T.fo[:, 0:2]), "su")
+    inc(V.tensor_tensor(T.t0[:], T.pxy[:], T.dxy[:], op.subtract), "su")
+    wait(V, "su")
+    inc(V.tensor_scalar(slot(0), T.t0[:], float(SHIFT), None, op.add), "su")
+    for l in range(2):
+        inc(V.tensor_scalar(T.band[:, 2 * BW * l:2 * BW * (l + 1)], T.dm[:], T.ff[:, l:l + 1], None, op.mult), "su")
+    wait(PE, "su")
+
+    steps = [
+        (T.w0, 0, ["lw0"], 1, 0, 2),
+        (T.w1, 1, w1_sems, 2, 1, None),
+        (T.v0, 2, ["av0"], 3, 4, 5),
+        (T.v1, 3, ["av1"], 5, 3, 6),
+        (T.w0, 0, [], 6, 5, 7),
+        (T.w1, 1, [], 7, 6, None),
+        (T.v0, 2, [], 8, 9, None),
+        (T.v1, 3, [], None, None, None),
+    ]
+    ps = (T.psx, T.psy)
+    H = R // 2
+    free_dv = [None]
+
+    for s, (win, bi, arr, sn, so, snew) in enumerate(steps):
+        landed = {2: 0, 6: 1}.get(s)
+        leaving = {1: 0, 5: 1}.get(s)
+        before = {0: 0, 4: 1}.get(s)
+        P0 = s * R
+        if landed is None:
+            offs, o0 = T.off, s * K
+        else:
+            offs, o0 = T["mi%d" % landed], 0
+        ka = 36 if landed is not None else 32
+
+        for q in (A, V):
+            if landed is None:
+                wait(q, "dv")
+            else:
+                wait(q, "am%d" % landed)
+        if landed is not None:
+            inc(V.tensor_copy(T.pos[:, 2 * K * sn:2 * K * (sn + 2)], offs[:, K:5 * K]), "cv")
+        for q in (A, V):
+            for nm in arr:
+                wait(q, nm)
+        inc(A.activation(T.p[:, P0:P0 + 16 * ka], win[:, 0:C].indirect(offs[:, o0:o0 + ka]),
+                         ActivationFunctionType.Copy), "ga")
+        inc(V.tensor_copy(T.p[:, P0 + 16 * ka:P0 + R], win[:, 0:C].indirect(offs[:, o0 + ka:o0 + K])), "gd")
+        if s == 7:
+            break
+
+        if free_dv[0] is not None:
+            PE.wait_ge(S.dv, free_dv[0])
+            wait(PE, "dx")
+        if landed is not None:
+            wait(PE, "cv")
+        if s == 2:
+            wait(PE, "ep")
+        for a in range(2):
+            PE.matmul(ps[a][:, 0:K], T.ib[:], T.kap[:], True, False)
+            PE.matmul(ps[a][:, 0:K], T.i2[:], slot(sn, a), False, False)
+            PE.matmul(ps[a][:, 0:K], T.im[:], slot(so, a), False, False)
+        wait(PE, "ga")
+        wait(PE, "gd")
+        for a in range(2):
+            b0 = (2 * bi + a) * BW + 15 + a
+            for i in range(16):
+                mm = PE.matmul(ps[a][:, 0:K], T.band[:, b0 - i:b0 - i + 128], T.p[:, P0 + i:P0 + R:16], False, i == 15)
+            inc(mm, "mx" if a == 0 else "my")
+        acc = (T.apa, T.apb) if 2 <= s <= 5 else (T.aoa, T.aob)
+        for hf in range(2):
+            mm = PE.matmul(acc[hf][:], T.ib[:], T.p[:, P0 + H * hf:P0 + H * (hf + 1)], s in (0, 2), s == 5)
+        if s == 5:
+            inc(mm, "ac")
+
+        for a in range(2):
+            wait(V, "mx" if a == 0 else "my")
+            inc(V.tensor_scalar(T.z[:, K * a:K * (a + 1)], ps[a][:, 0:K], 128.0, 63.5 + 128.0 * (1024 - SHIFT),
+                                op.mult, op.add), "dv")
+            outs = []
+            if snew is not None:
+                outs.append(slot(snew, a))
+            if leaving is not None:
+                outs.append(T["mo%d" % leaving][:, K * (1 + a):K * (2 + a)])
+            if before is not None:
+                outs.append(T["mo%d" % before][:, K * (3 + a):K * (4 + a)])
+            for o in outs:
+                inc(V.tensor_scalar(o, ps[a][:, 0:K], ROUND, -ROUND, op.add, op.add), "dx")
+            wait(V, "dv")
+            if a == 0:
+                inc(V.tensor_scalar(T.cc[:, 0:K], T.z[:, 0:K], 11, 63, op.arith_shift_right, op.bitwise_and), "dv")
+            else:
+                free_dv[0] = cnt["dv"]
+                inc(V.tensor_scalar(T.cc[:, K:2 * K], T.z[:, K:2 * K], 5, 63 * 64,
+                                    op.arith_shift_right, op.bitwise_and), "dv")
+        wait(V, "dv")
+        inc(V.tensor_tensor(T.cs[:], T.cc[:, 0:K], T.cc[:, K:2 * K], op.add), "dv")
+        wait(V, "dv")
+        if leaving is None:
+            inc(V.tensor_copy(T.off[:, (s + 1) * K:(s + 2) * K], T.cs[:]), "dv")
+        else:
+            inc(V.tensor_copy(T["mo%d" % leaving][:, 0:K], T.cs[:]), "dv")
+            wait(g, "dx")
+            wait(g, "dv")
+            send(g, topo, partner, T["mi%d" % leaving][:], T["mo%d" % leaving][:], S["am%d" % leaving], S.sent, lo)
+            cnt["sent"] += bits(lo)
+
+        if s == 1:
+            wait(V, "af")
+            inc(V.tensor_copy(T.ff[:, 2:3], T.fp0[:, 0:1]), "ep")
+            inc(V.tensor_copy(T.ff[:, 3:4], T.fp1[:, 0:1]), "ep")
+            wait(V, "ep")
+            for l in (2, 3):
+                inc(V.tensor_scalar(T.band[:, 2 * BW * l:2 * BW * (l + 1)], T.dm[:], T.ff[:, l:l + 1], None, op.mult), "ep")
+        if s == 5:
+            wait(V, "ac")
+            for hf, (bank, ev, arrive) in enumerate(((T.apa, "eva", "apa_in"), (T.apb, "evb", "apb_in"))):
+                inc(V.tensor_copy(T.po[:, H * hf:H * (hf + 1)], bank[:]), ev)
+                wait(g, ev)
+                send(g, topo, partner, T.pin[:, H * hf:H * (hf + 1)], T.po[:, H * hf:H * (hf + 1)], S[arrive], S.sent, lo)
+                cnt["sent"] += bits(lo)
+
+    P0 = 7 * R
+    wait(PE, "apa_in")
+    PE.matmul(T.aoa[:], T.ih[:], T.pin[:, 0:H], False, False)
+    wait(PE, "ga")
+    inc(PE.matmul(T.aoa[:], T.ib[:], T.p[:, P0:P0 + H], False, True), "fa")
+    wait(PE, "gd")
+    PE.matmul(T.aob[:], T.ib[:], T.p[:, P0 + H:P0 + R], False, False)
+    wait(PE, "apb_in")
+    inc(PE.matmul(T.aob[:], T.ih[:], T.pin[:, H:R], False, True), "fb")
+    wait(A, "fa")
+    inc(A.activation(T.yo[:, 0:H], T.aoa[:], ActivationFunctionType.Copy), "ya")
+    wait(A, "ya")
+    inc(A.dma_start(T.y[:, 0:H], T.yo[:, 0:H]), "sa", 16)
+    wait(V, "fb")
+    inc(V.tensor_copy(T.yo[:, H:R], T.aob[:]), "yb")
+    wait(SY, "yb")
+    inc(SY.dma_start(T.y[:, H:R], T.yo[:, H:R]), "sb", 16)
+    wait(g, "sent")
+    wait(A, "sa")
+    wait(SY, "sb")

@@ -7,7 +7,8 @@ K = R // 16
 BW = 144
 PIECES = [(0, 1344), (1344, 2720), (2720, C)]
 ROUND = 12582912.0
-KAPPA = -127.0 / 256.0
+ROUND64 = 805306368.0
+KAPPA = 1.0 / 4096
 SHIFT = 512
 
 SCRATCH = {
@@ -25,16 +26,22 @@ SCRATCH = {
     "pi": ("sbuf", [128, 8], "int32"),
     "pm": ("sbuf", [128, 8], "int32"),
     "mk": ("sbuf", [128, 8], "float32"),
-    "dg": ("sbuf", [128, BW], "float32"),
+    "dg": ("sbuf", [128, BW], "bfloat16"),
     "dm": ("sbuf", [128, 2 * BW], "bfloat16"),
+    "d3": ("sbuf", [128, 3 * BW], "bfloat16"),
     "band": ("sbuf", [128, 8 * BW], "bfloat16"),
     "ib": ("sbuf", [128, 128], "bfloat16"),
     "ih": ("sbuf", [128, 128], "float16"),
     "i2": ("sbuf", [128, 128], "float16"),
     "im": ("sbuf", [128, 128], "float16"),
+    "mv": ("sbuf", [128, 6 * 128], "float16"),
+    "mm": ("sbuf", [128, 4 * 128], "float16"),
     "kap": ("sbuf", [128, K], "bfloat16"),
+    "first": ("sbuf", [128, 4 * K], "float16"),
     "pos": ("sbuf", [128, 10 * 2 * K], "float16"),
-    "z": ("sbuf", [128, 2 * K], "int32"),
+    "rw": ("sbuf", [128, 4 * K], "float16"),
+    "tmp": ("sbuf", [128, 7 * 2 * K], "float32"),
+    "z": ("sbuf", [128, K], "int32"),
     "cc": ("sbuf", [128, 2 * K], "int32"),
     "cs": ("sbuf", [128, K], "int32"),
     "t0": ("sbuf", [128, 2 * K], "int32"),
@@ -46,16 +53,18 @@ SCRATCH = {
     "po": ("sbuf", [128, R], "float16"),
     "pin": ("sbuf", [128, R], "float16"),
     "yo": ("sbuf", [128, R], "float32"),
-    "psx": ("psum", [128, 512], "float32"),
-    "psy": ("psum", [128, 512], "float32"),
+    "psa": ("psum", [128, 512], "float32"),
+    "psb": ("psum", [128, 512], "float32"),
+    "pso": ("psum", [128, 512], "float32"),
+    "psi": ("psum", [128, 512], "float32"),
     "aoa": ("psum", [128, 512], "float32"),
     "aob": ("psum", [128, 512], "float32"),
     "apa": ("psum", [128, 512], "float32"),
     "apb": ("psum", [128, 512], "float32"),
 }
 SEMAPHORES = [
-    "lp", "ld", "lf", "lw0", "lw1a", "lw1b", "lw1c", "gi", "su", "dv", "dx", "ga", "gd", "mx", "my", "ep", "cv",
-    "ac", "eva", "evb", "fa", "fb", "ya", "yb", "sa", "sb", "sent",
+    "lp", "ld", "lf", "lw0", "lw1a", "lw1b", "lw1c", "gi", "su", "dv", "dx", "ga", "gd", "mx", "my", "ep", "eo", "cv",
+    "ra", "rb", "tm", "s2", "dm", "si", "ac", "eva", "evb", "fa", "fb", "ya", "yb", "sa", "sb", "sent",
     "af", "av0", "av1", "am0", "am1", "apa_in", "apb_in", "hf", "h0", "h1", "h2",
 ]
 
@@ -113,6 +122,7 @@ def rank_program(g, core, T, topo):
     S = T.sem
     V, A, PE, SY = g.vector, g.scalar, g.tensor, g.sync
     op = AluOpType
+    Copy = ActivationFunctionType.Copy
     _s, nxt, helper, lo, hi = rts[rank]
     prev, _me, phelper, plo, phi = rts[(rank - 1) % n]
     partner = rts[(rank + 2) % n][0]
@@ -154,14 +164,26 @@ def rank_program(g, core, T, topo):
     inc(V.memset(T.kap[:], KAPPA), "su")
     wait(V, "gi")
     inc(V.tensor_scalar(T.pm[:, 0:1], T.pi[:, 0:1], 15, None, op.bitwise_and), "su")
-    for buf, val in ((T.ib, 1.0), (T.ih, 1.0), (T.i2, 2.0), (T.im, -1.0)):
+    for buf, val in ((T.ib, 1.0), (T.i2, 2.0 / 16), (T.im, -1.0 / 16)):
         inc(V.tensor_scalar(buf[:], T.dg[:, 0:128], -1.0, val, op.is_equal, op.mult), "su")
     wait(V, "su")
     for a in range(2):
-        inc(V.tensor_scalar(T.mk[:, a:a + 1], T.pm[:, 0:1], float(14 + a), 1.0 / 128, op.is_equal, op.mult), "su")
+        inc(V.tensor_scalar(T.mk[:, a:a + 1], T.pm[:, 0:1], float(14 + a), 1.0 / 2048, op.is_equal, op.mult), "su")
+    for col, cmp, val in ((2, op.is_lt, 1.0), (3, op.is_ge, 1.0), (4, op.is_lt, 64.0), (5, op.is_ge, 64.0)):
+        inc(V.tensor_scalar(T.mk[:, col:col + 1], T.pm[:, 0:1], 8.0, val, cmp, op.mult), "su")
+    wait(V, "su")
+    for k, (diag, col) in enumerate(((0.0, 0), (7.0, 1), (-9.0, 1))):
+        inc(V.tensor_scalar(T.d3[:, k * BW:(k + 1) * BW], T.dg[:], diag, T.mk[:, col:col + 1], op.is_equal, op.mult), "su")
+    for k, (diag, col) in enumerate(((-1.0, 2), (7.0, 2), (-1.0, 3), (-9.0, 3), (-9.0, 5), (7.0, 4))):
+        inc(V.tensor_scalar(T.mv[:, 128 * k:128 * (k + 1)], T.dg[:, 0:128], diag, T.mk[:, col:col + 1],
+                            op.is_equal, op.mult), "su")
     wait(V, "su")
     for a in range(2):
-        inc(V.tensor_scalar(T.dm[:, a * BW:(a + 1) * BW], T.dg[:], 0.0, T.mk[:, a:a + 1], op.is_equal, op.mult), "su")
+        inc(V.tensor_tensor(T.dm[:, a * BW:(a + 1) * BW], T.d3[:, 0:BW], T.d3[:, (1 + a) * BW:(2 + a) * BW], op.add), "su")
+        inc(V.tensor_tensor(T.mm[:, 128 * a:128 * (a + 1)], T.mv[:, 256 * a:256 * a + 128],
+                            T.mv[:, 128 * (4 + a):128 * (5 + a)], op.add), "su")
+    wait(V, "su")
+    inc(V.tensor_scalar(T.mm[:, 256:512], T.mm[:, 0:256], -1.0, None, op.mult), "su")
 
     def dst_of(c):
         rid, pid, _se = topo.addr(c)
@@ -190,24 +212,35 @@ def rank_program(g, core, T, topo):
             return T.pos[:, 2 * K * k:2 * K * (k + 1)]
         return T.pos[:, 2 * K * k + K * a:2 * K * k + K * (a + 1)]
 
+    wait(V, "lf")
+    inc(V.tensor_copy(T.ff[:, 0:2], T.fo[:, 0:2]), "su")
+    wait(V, "su")
+    wait(A, "su")
+    for l in range(2):
+        inc(A.activation(T.band[:, 2 * BW * l:2 * BW * (l + 1)], T.dm[:], Copy, scale=T.ff[:, l:l + 1]), "eo")
     wait(V, "lp")
+    wait(V, "ld")
+    inc(V.tensor_tensor(T.t0[:], T.pxy[:], T.dxy[:], op.subtract), "su")
+    inc(V.tensor_scalar(T.first[:, 2 * K:4 * K], T.pxy[:], float(SHIFT), None, op.add), "su")
     inc(V.tensor_scalar(T.cc[:], T.pxy[:], 4, None, op.arith_shift_right), "dv")
-    inc(V.tensor_scalar(slot(1), T.pxy[:], float(SHIFT), None, op.add), "su")
+    wait(V, "su")
+    inc(V.tensor_scalar(T.first[:, 0:2 * K], T.t0[:], float(SHIFT), None, op.add), "su")
     wait(V, "dv")
-    inc(V.tensor_scalar(T.z[:, K:2 * K], T.cc[:, K:2 * K], 64.0, None, op.mult), "dv")
+    inc(V.tensor_scalar(T.z[:], T.cc[:, K:2 * K], 64.0, None, op.mult), "dv")
     wait(V, "dv")
-    inc(V.tensor_tensor(T.cs[:], T.cc[:, 0:K], T.z[:, K:2 * K], op.add), "dv")
+    inc(V.tensor_tensor(T.cs[:], T.cc[:, 0:K], T.z[:], op.add), "dv")
     wait(V, "dv")
     inc(V.tensor_copy(T.off[:, 0:K], T.cs[:]), "dv")
-    wait(V, "lf")
-    wait(V, "ld")
-    inc(V.tensor_copy(T.ff[:, 0:2], T.fo[:, 0:2]), "su")
-    inc(V.tensor_tensor(T.t0[:], T.pxy[:], T.dxy[:], op.subtract), "su")
-    wait(V, "su")
-    inc(V.tensor_scalar(slot(0), T.t0[:], float(SHIFT), None, op.add), "su")
-    for l in range(2):
-        inc(V.tensor_scalar(T.band[:, 2 * BW * l:2 * BW * (l + 1)], T.dm[:], T.ff[:, l:l + 1], None, op.mult), "su")
     wait(PE, "su")
+    for k in range(2):
+        for a in range(2):
+            o = T.psi[:, 2 * K * k + K * a:2 * K * k + K * (a + 1)]
+            PE.matmul(o, T.mv[:, 256 * a:256 * a + 128], T.first[:, 2 * K * k:2 * K * k + K], True, False)
+            mm = PE.matmul(o, T.mv[:, 256 * a + 128:256 * a + 256], T.first[:, 2 * K * k + K:2 * K * (k + 1)], False, True)
+    inc(mm, "si")
+    wait(V, "si")
+    inc(V.tensor_copy(T.pos[:, 0:4 * K], T.psi[:, 0:4 * K]), "dx")
+    wait(PE, "eo")
 
     steps = [
         (T.w0, 0, ["lw0"], 1, 0, 2),
@@ -219,9 +252,9 @@ def rank_program(g, core, T, topo):
         (T.v0, 2, [], 8, 9, None),
         (T.v1, 3, [], None, None, None),
     ]
-    ps = (T.psx, T.psy)
+    ps = (T.psa, T.psb)
     H = R // 2
-    free_dv = [None]
+    late = []
 
     for s, (win, bi, arr, sn, so, snew) in enumerate(steps):
         landed = {2: 0, 6: 1}.get(s)
@@ -232,7 +265,7 @@ def rank_program(g, core, T, topo):
             offs, o0 = T.off, s * K
         else:
             offs, o0 = T["mi%d" % landed], 0
-        ka = 36 if landed is not None else 32
+        ka = {0: 32, 2: 36, 6: 36, 7: 32}.get(s, 34)
 
         for q in (A, V):
             if landed is None:
@@ -244,15 +277,15 @@ def rank_program(g, core, T, topo):
         for q in (A, V):
             for nm in arr:
                 wait(q, nm)
-        inc(A.activation(T.p[:, P0:P0 + 16 * ka], win[:, 0:C].indirect(offs[:, o0:o0 + ka]),
-                         ActivationFunctionType.Copy), "ga")
+        inc(A.activation(T.p[:, P0:P0 + 16 * ka], win[:, 0:C].indirect(offs[:, o0:o0 + ka]), Copy), "ga")
         inc(V.tensor_copy(T.p[:, P0 + 16 * ka:P0 + R], win[:, 0:C].indirect(offs[:, o0 + ka:o0 + K])), "gd")
         if s == 7:
             break
+        for o, t in late:
+            inc(V.tensor_scalar(o, t, ROUND, -ROUND, op.add, op.add), "dm")
+        del late[:]
 
-        if free_dv[0] is not None:
-            PE.wait_ge(S.dv, free_dv[0])
-            wait(PE, "dx")
+        wait(PE, "dx")
         if landed is not None:
             wait(PE, "cv")
         if s == 2:
@@ -264,43 +297,47 @@ def rank_program(g, core, T, topo):
         wait(PE, "ga")
         wait(PE, "gd")
         for a in range(2):
-            b0 = (2 * bi + a) * BW + 15 + a
-            for i in range(16):
-                mm = PE.matmul(ps[a][:, 0:K], T.band[:, b0 - i:b0 - i + 128], T.p[:, P0 + i:P0 + R:16], False, i == 15)
+            b0 = (2 * bi + a) * BW + 15
+            for i in range(8 * a, 8 * a + 8):
+                mm = PE.matmul(ps[a][:, 0:K], T.band[:, b0 - i:b0 - i + 128], T.p[:, P0 + i:P0 + R:16], False, i % 8 == 7)
             inc(mm, "mx" if a == 0 else "my")
+
+        for a in range(2):
+            wait(V, "mx" if a == 0 else "my")
+            nm = "ra" if a == 0 else "rb"
+            inc(V.tensor_scalar(T.rw[:, 2 * K * a:2 * K * a + K], ps[a][:, 0:K], 1023.5, None, op.add), nm)
+            inc(V.tensor_scalar(T.rw[:, 2 * K * a + K:2 * K * (a + 1)], ps[a][:, 0:K], ROUND64, -ROUND64,
+                                op.add, op.add), nm)
+        both = T.tmp[:, 2 * K * s:2 * K * (s + 1)]
+        if s != 6:
+            for a in range(2):
+                inc(V.tensor_scalar(T.tmp[:, 2 * K * s + K * a:2 * K * s + K * (a + 1)], ps[a][:, 0:K], 16.0, -0.5,
+                                    op.mult, op.add), "tm")
+        if leaving is not None:
+            wait(V, "tm")
+            inc(V.tensor_scalar(T["mo%d" % leaving][:, K:3 * K], both, ROUND, -ROUND, op.add, op.add), "dx")
+
+        for a in range(2):
+            wait(PE, "ra" if a == 0 else "rb")
+            PE.matmul(T.pso[:, 0:K], T.mm[:, 128 * a:128 * (a + 1)], T.rw[:, 2 * K * a:2 * K * a + K], a == 0, False)
+            mm = PE.matmul(T.pso[:, 0:K], T.mm[:, 128 * (2 + a):128 * (3 + a)], T.rw[:, 2 * K * a + K:2 * K * (a + 1)],
+                           False, a == 1)
+        inc(mm, "s2")
         acc = (T.apa, T.apb) if 2 <= s <= 5 else (T.aoa, T.aob)
         for hf in range(2):
             mm = PE.matmul(acc[hf][:], T.ib[:], T.p[:, P0 + H * hf:P0 + H * (hf + 1)], s in (0, 2), s == 5)
         if s == 5:
             inc(mm, "ac")
-
-        for a in range(2):
-            wait(V, "mx" if a == 0 else "my")
-            inc(V.tensor_scalar(T.z[:, K * a:K * (a + 1)], ps[a][:, 0:K], 128.0, 63.5 + 128.0 * (1024 - SHIFT),
-                                op.mult, op.add), "dv")
-            outs = []
-            if snew is not None:
-                outs.append(slot(snew, a))
-            if leaving is not None:
-                outs.append(T["mo%d" % leaving][:, K * (1 + a):K * (2 + a)])
-            if before is not None:
-                outs.append(T["mo%d" % before][:, K * (3 + a):K * (4 + a)])
-            for o in outs:
-                inc(V.tensor_scalar(o, ps[a][:, 0:K], ROUND, -ROUND, op.add, op.add), "dx")
-            wait(V, "dv")
-            if a == 0:
-                inc(V.tensor_scalar(T.cc[:, 0:K], T.z[:, 0:K], 11, 63, op.arith_shift_right, op.bitwise_and), "dv")
-            else:
-                free_dv[0] = cnt["dv"]
-                inc(V.tensor_scalar(T.cc[:, K:2 * K], T.z[:, K:2 * K], 5, 63 * 64,
-                                    op.arith_shift_right, op.bitwise_and), "dv")
-        wait(V, "dv")
-        inc(V.tensor_tensor(T.cs[:], T.cc[:, 0:K], T.cc[:, K:2 * K], op.add), "dv")
-        wait(V, "dv")
-        if leaving is None:
-            inc(V.tensor_copy(T.off[:, (s + 1) * K:(s + 2) * K], T.cs[:]), "dv")
-        else:
-            inc(V.tensor_copy(T["mo%d" % leaving][:, 0:K], T.cs[:]), "dv")
+        wait(V, "s2")
+        o = T.off[:, (s + 1) * K:(s + 2) * K] if leaving is None else T["mo%d" % leaving][:, 0:K]
+        inc(V.tensor_scalar(o, T.pso[:, 0:K], -65.0 * (1024 - SHIFT // 16), None, op.add), "dv")
+        if snew is not None:
+            wait(V, "tm")
+            inc(V.tensor_scalar(slot(snew), both, ROUND, -ROUND, op.add, op.add), "dx")
+        if before is not None:
+            late.append((T["mo%d" % before][:, 3 * K:5 * K], both))
+        if leaving is not None:
+            wait(g, "dm")
             wait(g, "dx")
             wait(g, "dv")
             send(g, topo, partner, T["mi%d" % leaving][:], T["mo%d" % leaving][:], S["am%d" % leaving], S.sent, lo)
@@ -310,6 +347,7 @@ def rank_program(g, core, T, topo):
             wait(V, "af")
             inc(V.tensor_copy(T.ff[:, 2:3], T.fp0[:, 0:1]), "ep")
             inc(V.tensor_copy(T.ff[:, 3:4], T.fp1[:, 0:1]), "ep")
+            inc(V.tensor_scalar(T.ih[:], T.dg[:, 0:128], -1.0, 1.0, op.is_equal, op.mult), "ep")
             wait(V, "ep")
             for l in (2, 3):
                 inc(V.tensor_scalar(T.band[:, 2 * BW * l:2 * BW * (l + 1)], T.dm[:], T.ff[:, l:l + 1], None, op.mult), "ep")
@@ -331,7 +369,7 @@ def rank_program(g, core, T, topo):
     wait(PE, "apb_in")
     inc(PE.matmul(T.aob[:], T.ih[:], T.pin[:, H:R], False, True), "fb")
     wait(A, "fa")
-    inc(A.activation(T.yo[:, 0:H], T.aoa[:], ActivationFunctionType.Copy), "ya")
+    inc(A.activation(T.yo[:, 0:H], T.aoa[:], Copy), "ya")
     wait(A, "ya")
     inc(A.dma_start(T.y[:, 0:H], T.yo[:, 0:H]), "sa", 16)
     wait(V, "fb")

@@ -1,132 +1,106 @@
-from concourse.bass import DstId, RemoteDMATransfer
 from concourse.mybir import AluOpType, ActivationFunctionType
 
 C = 4096
+CF = C + 2
 R = 1024
+H = R // 2
 K = R // 16
-BW = 144
-PIECES = [(0, 1344), (1344, 2720), (2720, C)]
-ROUND = 12582912.0
-ROUND64 = 805306368.0
-KAPPA = 1.0 / 4096
+KB = K // 2
+BW = 136
+M = KB + 2 * K
+STEPS = 8
+FLOOR = 8388607.5
+ROUND1024 = 12884901888.0
+KAPPA = 1.0 / 256
 SHIFT = 512
+OPT = {"kv": 8, "kv0": 16, "kvl": 16, "early1": False, "cut": C}
 
 SCRATCH = {
-    "w0": ("sbuf", [128, C], "bfloat16"),
+    "w0": ("sbuf", [128, C + 16], "bfloat16"),
     "w1": ("sbuf", [128, C], "bfloat16"),
-    "v0": ("sbuf", [128, C], "bfloat16"),
+    "v0": ("sbuf", [128, C + 16], "bfloat16"),
     "v1": ("sbuf", [128, C], "bfloat16"),
-    "p": ("sbuf", [128, 8 * R], "bfloat16"),
-    "pxy": ("sbuf", [128, 2 * K], "int32"),
+    "p": ("sbuf", [128, STEPS * R], "bfloat16"),
+    "pxy": ("sbuf", [128, 4 * K], "int32"),
     "dxy": ("sbuf", [128, 2 * K], "int32"),
     "fo": ("sbuf", [128, 8], "int32"),
-    "fp0": ("sbuf", [128, 8], "int32"),
-    "fp1": ("sbuf", [128, 8], "int32"),
-    "ff": ("sbuf", [128, 8], "float32"),
     "pi": ("sbuf", [128, 8], "int32"),
     "pm": ("sbuf", [128, 8], "int32"),
-    "mk": ("sbuf", [128, 8], "float32"),
+    "mk": ("sbuf", [128, 16], "float32"),
+    "mb": ("sbuf", [128, 16], "bfloat16"),
     "dg": ("sbuf", [128, BW], "bfloat16"),
-    "dm": ("sbuf", [128, 2 * BW], "bfloat16"),
-    "d3": ("sbuf", [128, 3 * BW], "bfloat16"),
-    "band": ("sbuf", [128, 8 * BW], "bfloat16"),
+    "band": ("sbuf", [128, 4 * BW], "bfloat16"),
     "ib": ("sbuf", [128, 128], "bfloat16"),
-    "ih": ("sbuf", [128, 128], "float16"),
     "i2": ("sbuf", [128, 128], "float16"),
     "im": ("sbuf", [128, 128], "float16"),
-    "mv": ("sbuf", [128, 6 * 128], "float16"),
     "mm": ("sbuf", [128, 4 * 128], "float16"),
     "kap": ("sbuf", [128, K], "bfloat16"),
-    "first": ("sbuf", [128, 4 * K], "float16"),
-    "pos": ("sbuf", [128, 10 * 2 * K], "float16"),
+    "first": ("sbuf", [128, 8 * K], "float16"),
+    "pos": ("sbuf", [128, 32 * K], "float16"),
     "rw": ("sbuf", [128, 4 * K], "float16"),
-    "tmp": ("sbuf", [128, 7 * 2 * K], "float32"),
-    "z": ("sbuf", [128, K], "int32"),
-    "cc": ("sbuf", [128, 2 * K], "int32"),
-    "cs": ("sbuf", [128, K], "int32"),
-    "t0": ("sbuf", [128, 2 * K], "int32"),
-    "off": ("sbuf", [128, 8 * K], "uint16"),
-    "mo0": ("sbuf", [128, 5 * K], "uint16"),
-    "mo1": ("sbuf", [128, 5 * K], "uint16"),
-    "mi0": ("sbuf", [128, 5 * K], "uint16"),
-    "mi1": ("sbuf", [128, 5 * K], "uint16"),
+    "qx": ("sbuf", [128, K], "float16"),
+    "qy": ("sbuf", [128, K], "int32"),
+    "cs": ("sbuf", [128, K], "float32"),
+    "off": ("sbuf", [128, STEPS * K], "uint16"),
+    "mo": ("sbuf", [128, 4 * M], "uint16"),
+    "mi": ("sbuf", [128, 4 * M], "uint16"),
     "po": ("sbuf", [128, R], "float16"),
     "pin": ("sbuf", [128, R], "float16"),
     "yo": ("sbuf", [128, R], "float32"),
-    "psa": ("psum", [128, 512], "float32"),
-    "psb": ("psum", [128, 512], "float32"),
+    "se": ("sbuf", [128, R], "float32"),
+    "ps0": ("psum", [128, 512], "float32"),
+    "ps1": ("psum", [128, 512], "float32"),
     "pso": ("psum", [128, 512], "float32"),
-    "psi": ("psum", [128, 512], "float32"),
-    "aoa": ("psum", [128, 512], "float32"),
-    "aob": ("psum", [128, 512], "float32"),
-    "apa": ("psum", [128, 512], "float32"),
-    "apb": ("psum", [128, 512], "float32"),
+    "ao0": ("psum", [128, 512], "float32"),
+    "ao1": ("psum", [128, 512], "float32"),
+    "ao2": ("psum", [128, 512], "float32"),
+    "ap0": ("psum", [128, 512], "float32"),
+    "ap1": ("psum", [128, 512], "float32"),
 }
-SEMAPHORES = [
-    "lp", "ld", "lf", "lw0", "lw1a", "lw1b", "lw1c", "gi", "su", "dv", "dx", "ga", "gd", "mx", "my", "ep", "eo", "cv",
-    "ra", "rb", "tm", "s2", "dm", "si", "ac", "eva", "evb", "fa", "fb", "ya", "yb", "sa", "sb", "sent",
-    "af", "av0", "av1", "am0", "am1", "apa_in", "apb_in", "hf", "h0", "h1", "h2",
-]
+SEMAPHORES = (["lp", "ld", "lf", "gi", "su", "si", "ep", "sent", "sa", "sb", "fz", "ya", "yb", "yc", "f0", "f1", "f2"]
+              + [a + str(b) for a in ("dv", "dx", "ga", "gd", "mx", "rr", "ww", "s2", "cv", "ac", "ev", "eb", "av", "pa")
+                 for b in range(2)]
+              + [a + str(b) for a in ("lw", "am") for b in range(6)])
 
 
 def bits(m):
     return bin(m).count("1")
 
 
-def relay_core(src, dst, cores, topo):
-    for h in topo.cores_of(src):
-        if h not in cores and topo.die(h) != topo.die(src) and topo.may_write(h, dst):
-            return h
-    return None
-
-
-def routes(T, topo):
+def plan(T, topo, r):
     cores = list(T.cores)
     n = len(cores)
-    out = []
-    for r in range(n):
-        s, d, partner = cores[r], cores[(r + 1) % n], cores[(r + 2) % n]
-        near = [c for c in topo.cores_of(s) if c != s][0]
-        lo = topo.mask(s, partner)
-        hi = topo.mask(s, near) & ~lo
-        h = None if topo.chip(s) == topo.chip(d) else relay_core(s, d, cores, topo)
-        out.append((s, d, h, lo, hi))
-    return out
+    if topo.chip(cores[r]) == topo.chip(cores[(r + 1) % n]):
+        return (r + 1) % n, [(r, 0, [0, 1, 2, 3]), ((r + 2) % n, 4, [0, 1, 2, 3])]
+    return (r - 1) % n, [(r, 0, [0, 1]), ((r + 2) % n, 2, [2, 3, 0, 1]), (r, 6, [2, 3])]
 
 
-def send(g, topo, dst, out_ap, in_ap, rsem, lsem, mask):
-    rid, pid, _se = topo.addr(dst)
-    g.remote_dma(out_ap, in_ap, rsem, lsem, pid, rid, mask)
-
-
-def relay_program(g, core, d, hi, T, topo):
-    S = T.sem
-    m = topo.mask(core, d)
-    g.wait_ge(S.hf, bits(hi))
-    send(g, topo, d, T.fp1[:, 0:1], T.fp1[:, 0:1], S.af, S.sent, m)
-    for k, (a, b) in enumerate(PIECES):
-        g.wait_ge(S["h%d" % k], bits(hi))
-        send(g, topo, d, T.v1[:, a:b], T.v1[:, a:b], S.av1, S.sent, m)
-    g.wait_ge(S.sent, bits(m) * (1 + len(PIECES)))
+def bulk(T, topo, r):
+    cores = list(T.cores)
+    twin, phases = plan(T, topo, r)
+    full = topo.mask(cores[r], cores[twin])
+    spare = full & ~topo.mask(cores[r], cores[(r + 2) % len(cores)])
+    cut = OPT["cut"] if len(phases[0][2]) == 2 else C
+    out = [(0, 0, C // 2, full), (0, C // 2, CF, full), (1, 0, cut, full), (1, cut, C, spare)]
+    return [x for x in out if x[1] < x[2]]
 
 
 def rank_program(g, core, T, topo):
     rank = T.rank_of(core)
-    rts = routes(T, topo)
     if rank is None:
-        for (s, d, h, lo, hi) in rts:
-            if h == core:
-                relay_program(g, core, d, hi, T, topo)
         return
-    n = len(rts)
+    cores = list(T.cores)
+    n = len(cores)
     S = T.sem
     V, A, PE, SY = g.vector, g.scalar, g.tensor, g.sync
     op = AluOpType
     Copy = ActivationFunctionType.Copy
-    _s, nxt, helper, lo, hi = rts[rank]
-    prev, _me, phelper, plo, phi = rts[(rank - 1) % n]
-    partner = rts[(rank + 2) % n][0]
-    cnt = {}
+    twin, phases = plan(T, topo, rank)
+    pieces = bulk(T, topo, rank)
+    partner = cores[(rank + 2) % n]
+    hop_mask = topo.mask(core, partner)
+    returns = phases[-1][0] != rank
+    cnt = {"sent": 0}
 
     def inc(ins, name, k=1):
         ins.then_inc(S[name], k)
@@ -135,247 +109,321 @@ def rank_program(g, core, T, topo):
     def wait(q, name):
         q.wait_ge(S[name], cnt[name])
 
-    hop_in = bits(topo.mask(partner, core))
-    if phelper is None:
-        cnt["af"] = bits(plo) + bits(phi)
-        cnt["av0"] = bits(plo | phi)
-        cnt["av1"] = bits(phi)
-    else:
-        cnt["af"] = bits(plo) + bits(topo.mask(phelper, core))
-        cnt["av0"] = bits(plo)
-        cnt["av1"] = bits(topo.mask(phelper, core)) * len(PIECES)
-    for nm in ("am0", "am1", "apa_in", "apb_in"):
-        cnt[nm] = hop_in
-    cnt["sent"] = 0
+    def remote(to, out_ap, in_ap, rsem, mask):
+        rid, pid, _se = topo.addr(to)
+        g.remote_dma(out_ap, in_ap, S[rsem], S.sent, pid, rid, mask)
+        cnt["sent"] += bits(mask)
 
-    inc(A.dma_start(T.fo[:, 0:2], T.fac[:]), "lf", 16)
+    for (l, a, b, m) in bulk(T, topo, twin):
+        cnt["av%d" % l] = cnt.get("av%d" % l, 0) + bits(m)
+    for bt in range(2):
+        cnt["pa%d" % bt] = bits(topo.mask(partner, core))
+        for k in range(1, len(phases)):
+            cnt["am%d" % (2 * k + bt)] = bits(topo.mask(partner, core))
+
     inc(SY.dma_start(T.pxy[:, 0:K], T.px[:]), "lp", 16)
     inc(A.dma_start(T.pxy[:, K:2 * K], T.py[:]), "lp", 16)
+    inc(A.dma_start(T.fo[:, 0:2], T.fac[:]), "lf", 16)
     inc(SY.dma_start(T.dxy[:, 0:K], T.dx[:]), "ld", 16)
     inc(A.dma_start(T.dxy[:, K:2 * K], T.dy[:]), "ld", 16)
-    inc(SY.dma_start(T.w0[:], T.lay[:, 0:C]), "lw0", 16)
-    w1_pieces = PIECES if helper is not None else [(0, C)]
-    w1_sems = ["lw1a", "lw1b", "lw1c"][:len(w1_pieces)]
-    for (a, b), nm in zip(w1_pieces, w1_sems):
-        inc(SY.dma_start(T.w1[:, a:b], T.lay[:, C + a:C + b]), nm, 16)
+    for k, (l, a, b, m) in enumerate(pieces):
+        b = min(b, C)
+        inc(SY.dma_start((T.w0, T.w1)[l][:, a:b], T.lay[:, C * l + a:C * l + b]), "lw%d" % k, 16)
+    arrive = {l: ["lw%d" % k for k, x in enumerate(pieces) if x[0] == l] for l in range(2)}
+    arrive.update({2: ["av0"], 3: ["av1"]})
 
-    inc(g.iota(T.dg[:], [[1, BW]], -1, -1, allow_small_or_imprecise_dtypes=True), "gi")
     inc(g.iota(T.pi[:, 0:1], [[1, 1]], 0, 1), "gi")
-    inc(V.memset(T.kap[:], KAPPA), "su")
     wait(V, "gi")
+    inc(g.iota(T.dg[:], [[1, BW]], 0, -1, allow_small_or_imprecise_dtypes=True), "gi")
     inc(V.tensor_scalar(T.pm[:, 0:1], T.pi[:, 0:1], 15, None, op.bitwise_and), "su")
-    for buf, val in ((T.ib, 1.0), (T.i2, 2.0 / 16), (T.im, -1.0 / 16)):
-        inc(V.tensor_scalar(buf[:], T.dg[:, 0:128], -1.0, val, op.is_equal, op.mult), "su")
+    inc(V.memset(T.kap[:], KAPPA), "su")
     wait(V, "su")
-    for a in range(2):
-        inc(V.tensor_scalar(T.mk[:, a:a + 1], T.pm[:, 0:1], float(14 + a), 1.0 / 2048, op.is_equal, op.mult), "su")
-    for col, cmp, val in ((2, op.is_lt, 1.0), (3, op.is_ge, 1.0), (4, op.is_lt, 64.0), (5, op.is_ge, 64.0)):
-        inc(V.tensor_scalar(T.mk[:, col:col + 1], T.pm[:, 0:1], 8.0, val, cmp, op.mult), "su")
+    col = {}
+    for k, (nm, s1, s2, o0, o1) in enumerate((
+            ("slope", 14.0, 1.0 / 128, op.is_ge, op.mult),
+            ("diag", 7.0, -105.0, op.mult, op.add),
+            ("down", 8.0, -8.0, op.is_ge, op.mult),
+            ("up", 8.0, 8.0, op.is_lt, op.mult),
+            ("low", 8.0, 1.0, op.is_lt, op.mult),
+            ("high", 8.0, 1.0 / 64, op.is_ge, op.mult),
+            ("h63", 8.0, 63.0, op.is_ge, op.mult))):
+        col[nm] = (T.mb if nm == "diag" else T.mk)[:, k:k + 1]
+        inc(V.tensor_scalar(col[nm], T.pm[:, 0:1], s1, s2, o0, o1), "su")
+    wait(V, "gi")
+    for buf, val in ((T.ib, 1.0), (T.i2, 2.0), (T.im, -1.0)):
+        inc(V.tensor_scalar(buf[:], T.dg[:, 0:128], 0.0, val, op.is_equal, op.mult), "su")
     wait(V, "su")
-    for k, (diag, col) in enumerate(((0.0, 0), (7.0, 1), (-9.0, 1))):
-        inc(V.tensor_scalar(T.d3[:, k * BW:(k + 1) * BW], T.dg[:], diag, T.mk[:, col:col + 1], op.is_equal, op.mult), "su")
-    for k, (diag, col) in enumerate(((-1.0, 2), (7.0, 2), (-1.0, 3), (-9.0, 3), (-9.0, 5), (7.0, 4))):
-        inc(V.tensor_scalar(T.mv[:, 128 * k:128 * (k + 1)], T.dg[:, 0:128], diag, T.mk[:, col:col + 1],
-                            op.is_equal, op.mult), "su")
+    col["wr"], col["ww"] = T.mk[:, 8:9], T.mk[:, 9:10]
+    inc(V.tensor_scalar(col["wr"], col["h63"], 1.0, None, op.add), "su")
+    inc(V.tensor_scalar(col["ww"], col["h63"], 1.0, -1.0 / 16, op.add, op.mult), "su")
     wait(V, "su")
-    for a in range(2):
-        inc(V.tensor_tensor(T.dm[:, a * BW:(a + 1) * BW], T.d3[:, 0:BW], T.d3[:, (1 + a) * BW:(2 + a) * BW], op.add), "su")
-        inc(V.tensor_tensor(T.mm[:, 128 * a:128 * (a + 1)], T.mv[:, 256 * a:256 * a + 128],
-                            T.mv[:, 128 * (4 + a):128 * (5 + a)], op.add), "su")
-    wait(V, "su")
-    inc(V.tensor_scalar(T.mm[:, 256:512], T.mm[:, 0:256], -1.0, None, op.mult), "su")
+    for k, (d, w) in enumerate((("down", "wr"), ("up", "wr"), ("down", "ww"), ("up", "ww"))):
+        inc(V.tensor_scalar(T.mm[:, 128 * k:128 * (k + 1)], T.dg[:, 0:128], col[d], col[w], op.is_equal, op.mult), "su")
 
-    def dst_of(c):
-        rid, pid, _se = topo.addr(c)
-        return DstId(rid=rid, pnc=pid)
-
-    second = nxt if helper is None else helper
-    wait(g, "lf")
-    g.remote_dma_fused([
-        RemoteDMATransfer(dst_ids=[dst_of(nxt)], dma_engine_mask=lo, remote_sem=S.af,
-                          src=T.fo[:, 0:1], dst=T.fp0[:, 0:1]),
-        RemoteDMATransfer(dst_ids=[dst_of(second)], dma_engine_mask=hi,
-                          remote_sem=S.af if helper is None else S.hf, src=T.fo[:, 1:2], dst=T.fp1[:, 0:1]),
-    ], local_sem=S.sent)
-    cnt["sent"] += bits(lo) + bits(hi)
-    wait(g, "lw0")
-    m0 = (lo | hi) if helper is None else lo
-    send(g, topo, nxt, T.v0[:], T.w0[:], S.av0, S.sent, m0)
-    cnt["sent"] += bits(m0)
-    for k, ((a, b), nm) in enumerate(zip(w1_pieces, w1_sems)):
-        wait(g, nm)
-        send(g, topo, second, T.v1[:, a:b], T.w1[:, a:b], S.av1 if helper is None else S["h%d" % k], S.sent, hi)
-        cnt["sent"] += bits(hi)
-
-    def slot(k, a=None):
-        if a is None:
-            return T.pos[:, 2 * K * k:2 * K * (k + 1)]
-        return T.pos[:, 2 * K * k + K * a:2 * K * k + K * (a + 1)]
-
-    wait(V, "lf")
-    inc(V.tensor_copy(T.ff[:, 0:2], T.fo[:, 0:2]), "su")
-    wait(V, "su")
-    wait(A, "su")
-    for l in range(2):
-        inc(A.activation(T.band[:, 2 * BW * l:2 * BW * (l + 1)], T.dm[:], Copy, scale=T.ff[:, l:l + 1]), "eo")
     wait(V, "lp")
+    inc(V.tensor_scalar(T.qx[:], T.pxy[:, 0:K], 1.0 / 64, 256.0 - 15.0 / 128, op.mult, op.add), "si")
+    inc(V.tensor_scalar(T.qy[:], T.pxy[:, K:2 * K], 1008, None, op.bitwise_and), "si")
+    wait(V, "lf")
+    inc(V.tensor_scalar(T.w0[:, C:CF], T.fo[:, 0:2], col["slope"], None, op.mult), "fz")
+    wait(V, "si")
+    inc(V.tensor_tensor(T.cs[:], T.qy[:], T.qx[:], op.add), "si")
     wait(V, "ld")
-    inc(V.tensor_tensor(T.t0[:], T.pxy[:], T.dxy[:], op.subtract), "su")
-    inc(V.tensor_scalar(T.first[:, 2 * K:4 * K], T.pxy[:], float(SHIFT), None, op.add), "su")
-    inc(V.tensor_scalar(T.cc[:], T.pxy[:], 4, None, op.arith_shift_right), "dv")
+    inc(V.tensor_tensor(T.pxy[:, 2 * K:4 * K], T.pxy[:, 0:2 * K], T.dxy[:], op.subtract), "su")
+    wait(V, "si")
+    inc(V.tensor_scalar(T.off[:, 0:K], T.cs[:], 4.0, -1024.0, op.mult, op.add), "dv0")
     wait(V, "su")
-    inc(V.tensor_scalar(T.first[:, 0:2 * K], T.t0[:], float(SHIFT), None, op.add), "su")
-    wait(V, "dv")
-    inc(V.tensor_scalar(T.z[:], T.cc[:, K:2 * K], 64.0, None, op.mult), "dv")
-    wait(V, "dv")
-    inc(V.tensor_tensor(T.cs[:], T.cc[:, 0:K], T.z[:], op.add), "dv")
-    wait(V, "dv")
-    inc(V.tensor_copy(T.off[:, 0:K], T.cs[:]), "dv")
+    for h, nm in enumerate(("low", "high")):
+        inc(V.tensor_scalar(T.first[:, 4 * K * h:4 * K * (h + 1)], T.pxy[:], float(SHIFT), col[nm], op.add, op.mult), "su")
+    wait(V, "fz")
+
+    def make_bands(l0, w):
+        for l in range(2):
+            inc(V.tensor_scalar(T.band[:, BW * (l0 + l):BW * (l0 + l + 1)], T.dg[:], col["diag"], w[:, C + l:C + l + 1],
+                                op.is_equal, op.mult), "ep")
+
+    make_bands(0, T.w0)
     wait(PE, "su")
-    for k in range(2):
-        for a in range(2):
-            o = T.psi[:, 2 * K * k + K * a:2 * K * k + K * (a + 1)]
-            PE.matmul(o, T.mv[:, 256 * a:256 * a + 128], T.first[:, 2 * K * k:2 * K * k + K], True, False)
-            mm = PE.matmul(o, T.mv[:, 256 * a + 128:256 * a + 256], T.first[:, 2 * K * k + K:2 * K * (k + 1)], False, True)
+    for h in range(2):
+        for k in range(2):
+            o = T.pso[:, 2 * K * h + K * k:2 * K * h + K * (k + 1)]
+            c0 = 4 * K * h + 2 * K * k
+            PE.matmul(o, T.mm[:, 0:128], T.first[:, c0:c0 + K], True, False)
+            mm = PE.matmul(o, T.mm[:, 128:256], T.first[:, c0 + K:c0 + 2 * K], False, True)
     inc(mm, "si")
     wait(V, "si")
-    inc(V.tensor_copy(T.pos[:, 0:4 * K], T.psi[:, 0:4 * K]), "dx")
-    wait(PE, "eo")
+    for h in range(2):
+        inc(V.tensor_copy(T.pos[:, h:4 * K:2], T.pso[:, 2 * K * h:2 * K * (h + 1)]), "dx0")
 
-    steps = [
-        (T.w0, 0, ["lw0"], 1, 0, 2),
-        (T.w1, 1, w1_sems, 2, 1, None),
-        (T.v0, 2, ["av0"], 3, 4, 5),
-        (T.v1, 3, ["av1"], 5, 3, 6),
-        (T.w0, 0, [], 6, 5, 7),
-        (T.w1, 1, [], 7, 6, None),
-        (T.v0, 2, [], 8, 9, None),
-        (T.v1, 3, [], None, None, None),
-    ]
-    ps = (T.psa, T.psb)
-    H = R // 2
-    late = []
+    for k, (l, a, b, m) in enumerate(pieces):
+        wait(g, "lw%d" % k)
+        if b > C:
+            wait(g, "fz")
+        remote(cores[twin], (T.v0, T.v1)[l][:, a:b], (T.w0, T.w1)[l][:, a:b], "av%d" % l, m)
 
-    for s, (win, bi, arr, sn, so, snew) in enumerate(steps):
-        landed = {2: 0, 6: 1}.get(s)
-        leaving = {1: 0, 5: 1}.get(s)
-        before = {0: 0, 4: 1}.get(s)
-        P0 = s * R
-        if landed is None:
-            offs, o0 = T.off, s * K
-        else:
-            offs, o0 = T["mi%d" % landed], 0
-        ka = {0: 32, 2: 36, 6: 36, 7: 32}.get(s, 34)
+    wins = (T.w0, T.w1, T.v0, T.v1)
+    ps = (T.ps0, T.ps1)
+    ap = (T.ap0, T.ap1)
+    place = {0: (0, 2 * K), 1: (K, 3 * K)}
+    free = [4 * K]
+    seen = {}
+    if returns:
+        own_banks = [(T.ao0, 0, H), (T.ao1, H, R)]
+    else:
+        own_banks = [(T.ao0, 0, H), (T.ao1, H, H + H // 2), (T.ao2, H + H // 2, R)]
+    own_all = sum(len(w) for (o, s0, w) in phases if o == rank) + int(not returns)
+    own_done = {0: 0, 1: 0}
 
-        for q in (A, V):
-            if landed is None:
-                wait(q, "dv")
+    def once(key):
+        new = key not in seen
+        seen[key] = 1
+        return new
+
+    def own_add(bt, lhs, buf, c0):
+        own_done[bt] += 1
+        for j, (bank, a, b) in enumerate(own_banks):
+            if a // H == bt:
+                mm = PE.matmul(bank[:, 0:b - a], lhs, buf[:, c0 + a:c0 + b], own_done[bt] == 1, own_done[bt] == own_all)
+                if own_done[bt] == own_all:
+                    inc(mm, "f%d" % j)
+
+    def send_sum(bt):
+        wait(g, "ev%d" % bt)
+        remote(partner, T.pin[:, H * bt:H * (bt + 1)], T.po[:, H * bt:H * (bt + 1)], "pa%d" % bt, hop_mask)
+
+    def run_phase(pk, base):
+        owner, s0, wl = phases[pk]
+        nh = 2 * len(wl)
+        hops = s0 + len(wl) < STEPS
+
+        def info(k):
+            bt, j = k % 2, k // 2
+            return bt, j, s0 + j, (base + j) * R + bt * H
+
+        def moves(k):
+            return 0 <= k < nh and info(k)[2] < STEPS - 1
+
+        def landed(k):
+            return k < 2 and pk > 0
+
+        def share(k):
+            if k == 0:
+                return OPT["kv0"]
+            if not moves(k):
+                return KB if owner != rank else OPT["kvl"] if k % 2 else OPT["kv"]
+            return OPT["kv"]
+
+        def gather(q, k):
+            bt, j, s, P0 = info(k)
+            if landed(k):
+                buf, o0, sem = T.mi, (2 * (pk - 1) + bt) * M, "am%d" % (2 * pk + bt)
             else:
-                wait(q, "am%d" % landed)
-        if landed is not None:
-            inc(V.tensor_copy(T.pos[:, 2 * K * sn:2 * K * (sn + 2)], offs[:, K:5 * K]), "cv")
-        for q in (A, V):
-            for nm in arr:
-                wait(q, nm)
-        inc(A.activation(T.p[:, P0:P0 + 16 * ka], win[:, 0:C].indirect(offs[:, o0:o0 + ka]), Copy), "ga")
-        inc(V.tensor_copy(T.p[:, P0 + 16 * ka:P0 + R], win[:, 0:C].indirect(offs[:, o0 + ka:o0 + K])), "gd")
-        if s == 7:
-            break
-        for o, t in late:
-            inc(V.tensor_scalar(o, t, ROUND, -ROUND, op.add, op.add), "dm")
-        del late[:]
+                buf, o0, sem = T.off, (base + j) * K + bt * KB, "dv%d" % (bt if s else 0)
+            ka = KB - share(k)
+            half = slice(H * bt, H * (bt + 1))
+            if q is A and not ka:
+                wait(A, "ac%d" % bt)
+                inc(A.activation(T.se[:, half], ap[bt][:], Copy), "eb%d" % bt)
+                return
+            wait(q, sem)
+            for nm in arrive[wl[j]]:
+                if once((nm, q is A)):
+                    wait(q, nm)
+            win = wins[wl[j]][:, 0:C]
+            if q is A:
+                inc(A.activation(T.p[:, P0:P0 + 16 * ka], win.indirect(buf[:, o0:o0 + ka]), Copy), "ga%d" % bt)
+            elif not ka:
+                wait(V, "eb%d" % bt)
+                inc(V.tensor_tensor(T.po[:, half], win.indirect(buf[:, o0:o0 + KB]), T.se[:, half], op.add), "ev%d" % bt)
+                send_sum(bt)
+            else:
+                inc(V.tensor_copy(T.p[:, P0 + 16 * ka:P0 + H], win.indirect(buf[:, o0 + ka:o0 + KB])), "gd%d" % bt)
+                if landed(k):
+                    c0 = free[0]
+                    free[0] += 2 * K
+                    place[bt] = (c0, c0 + K)
+                    inc(V.tensor_copy(T.pos[:, c0:c0 + 2 * K], buf[:, o0 + KB:o0 + M]), "cv%d" % bt)
+                if wl[j] == 2 and once("bands"):
+                    make_bands(2, T.v0)
 
-        wait(PE, "dx")
-        if landed is not None:
-            wait(PE, "cv")
-        if s == 2:
-            wait(PE, "ep")
-        for a in range(2):
-            PE.matmul(ps[a][:, 0:K], T.ib[:], T.kap[:], True, False)
-            PE.matmul(ps[a][:, 0:K], T.i2[:], slot(sn, a), False, False)
-            PE.matmul(ps[a][:, 0:K], T.im[:], slot(so, a), False, False)
-        wait(PE, "ga")
-        wait(PE, "gd")
-        for a in range(2):
-            b0 = (2 * bi + a) * BW + 15
-            for i in range(8 * a, 8 * a + 8):
-                mm = PE.matmul(ps[a][:, 0:K], T.band[:, b0 - i:b0 - i + 128], T.p[:, P0 + i:P0 + R:16], False, i % 8 == 7)
-            inc(mm, "mx" if a == 0 else "my")
+        def positions(k, stop):
+            bt = k % 2
+            a, b = place[bt]
+            PE.matmul(ps[bt][:, 0:K], T.i2[:], T.pos[:, a:a + K], False, False)
+            return PE.matmul(ps[bt][:, 0:K], T.im[:], T.pos[:, b:b + K], False, stop)
 
-        for a in range(2):
-            wait(V, "mx" if a == 0 else "my")
-            nm = "ra" if a == 0 else "rb"
-            inc(V.tensor_scalar(T.rw[:, 2 * K * a:2 * K * a + K], ps[a][:, 0:K], 1023.5, None, op.add), nm)
-            inc(V.tensor_scalar(T.rw[:, 2 * K * a + K:2 * K * (a + 1)], ps[a][:, 0:K], ROUND64, -ROUND64,
-                                op.add, op.add), nm)
-        both = T.tmp[:, 2 * K * s:2 * K * (s + 1)]
-        if s != 6:
-            for a in range(2):
-                inc(V.tensor_scalar(T.tmp[:, 2 * K * s + K * a:2 * K * s + K * (a + 1)], ps[a][:, 0:K], 16.0, -0.5,
-                                    op.mult, op.add), "tm")
-        if leaving is not None:
-            wait(V, "tm")
-            inc(V.tensor_scalar(T["mo%d" % leaving][:, K:3 * K], both, ROUND, -ROUND, op.add, op.add), "dx")
+        def open_bank(k):
+            bt = k % 2
+            if "dx%d" % bt in cnt:
+                wait(PE, "dx%d" % bt)
+            PE.matmul(ps[bt][:, 0:K], T.ib[:], T.kap[:], True, False)
+            if not landed(k):
+                positions(k, False)
 
-        for a in range(2):
-            wait(PE, "ra" if a == 0 else "rb")
-            PE.matmul(T.pso[:, 0:K], T.mm[:, 128 * a:128 * (a + 1)], T.rw[:, 2 * K * a:2 * K * a + K], a == 0, False)
-            mm = PE.matmul(T.pso[:, 0:K], T.mm[:, 128 * (2 + a):128 * (3 + a)], T.rw[:, 2 * K * a + K:2 * K * (a + 1)],
-                           False, a == 1)
-        inc(mm, "s2")
-        acc = (T.apa, T.apb) if 2 <= s <= 5 else (T.aoa, T.aob)
-        for hf in range(2):
-            mm = PE.matmul(acc[hf][:], T.ib[:], T.p[:, P0 + H * hf:P0 + H * (hf + 1)], s in (0, 2), s == 5)
-        if s == 5:
-            inc(mm, "ac")
-        wait(V, "s2")
-        o = T.off[:, (s + 1) * K:(s + 2) * K] if leaving is None else T["mo%d" % leaving][:, 0:K]
-        inc(V.tensor_scalar(o, T.pso[:, 0:K], -65.0 * (1024 - SHIFT // 16), None, op.add), "dv")
-        if snew is not None:
-            wait(V, "tm")
-            inc(V.tensor_scalar(slot(snew), both, ROUND, -ROUND, op.add, op.add), "dx")
-        if before is not None:
-            late.append((T["mo%d" % before][:, 3 * K:5 * K], both))
-        if leaving is not None:
-            wait(g, "dm")
-            wait(g, "dx")
-            wait(g, "dv")
-            send(g, topo, partner, T["mi%d" % leaving][:], T["mo%d" % leaving][:], S["am%d" % leaving], S.sent, lo)
-            cnt["sent"] += bits(lo)
+        def slopes(k):
+            bt, j, s, P0 = info(k)
+            if once(("band", wl[j] // 2)):
+                wait(PE, "ep")
+            wait(PE, "ga%d" % bt)
+            wait(PE, "gd%d" % bt)
+            b0 = BW * wl[j] + 7
+            for i in range(8):
+                mm = PE.matmul(ps[bt][:, 0:K], T.band[:, b0 - i:b0 - i + 128], T.p[:, P0 + i:P0 + H:8], False,
+                               i == 7 and not landed(k))
+            if landed(k):
+                wait(PE, "cv%d" % bt)
+                mm = positions(k, True)
+            inc(mm, "mx%d" % bt)
 
-        if s == 1:
-            wait(V, "af")
-            inc(V.tensor_copy(T.ff[:, 2:3], T.fp0[:, 0:1]), "ep")
-            inc(V.tensor_copy(T.ff[:, 3:4], T.fp1[:, 0:1]), "ep")
-            inc(V.tensor_scalar(T.ih[:], T.dg[:, 0:128], -1.0, 1.0, op.is_equal, op.mult), "ep")
-            wait(V, "ep")
-            for l in (2, 3):
-                inc(V.tensor_scalar(T.band[:, 2 * BW * l:2 * BW * (l + 1)], T.dm[:], T.ff[:, l:l + 1], None, op.mult), "ep")
-        if s == 5:
-            wait(V, "ac")
-            for hf, (bank, ev, arrive) in enumerate(((T.apa, "eva", "apa_in"), (T.apb, "evb", "apb_in"))):
-                inc(V.tensor_copy(T.po[:, H * hf:H * (hf + 1)], bank[:]), ev)
-                wait(g, ev)
-                send(g, topo, partner, T.pin[:, H * hf:H * (hf + 1)], T.po[:, H * hf:H * (hf + 1)], S[arrive], S.sent, lo)
-                cnt["sent"] += bits(lo)
+        def rounds(k):
+            bt = k % 2
+            wait(V, "mx%d" % bt)
+            inc(V.tensor_scalar(T.rw[:, 2 * K * bt:2 * K * bt + K], ps[bt][:, 0:K], 1.0 / 16, 1023.5, op.mult, op.add),
+                "rr%d" % bt)
+            inc(V.tensor_scalar(T.rw[:, 2 * K * bt + K:2 * K * (bt + 1)], ps[bt][:, 0:K], ROUND1024, -ROUND1024,
+                                op.add, op.add), "ww%d" % bt)
 
-    P0 = 7 * R
-    wait(PE, "apa_in")
-    PE.matmul(T.aoa[:], T.ih[:], T.pin[:, 0:H], False, False)
-    wait(PE, "ga")
-    inc(PE.matmul(T.aoa[:], T.ib[:], T.p[:, P0:P0 + H], False, True), "fa")
-    wait(PE, "gd")
-    PE.matmul(T.aob[:], T.ib[:], T.p[:, P0 + H:P0 + R], False, False)
-    wait(PE, "apb_in")
-    inc(PE.matmul(T.aob[:], T.ih[:], T.pin[:, H:R], False, True), "fb")
-    wait(A, "fa")
-    inc(A.activation(T.yo[:, 0:H], T.aoa[:], Copy), "ya")
-    wait(A, "ya")
-    inc(A.dma_start(T.y[:, 0:H], T.yo[:, 0:H]), "sa", 16)
-    wait(V, "fb")
-    inc(V.tensor_copy(T.yo[:, H:R], T.aob[:]), "yb")
-    wait(SY, "yb")
-    inc(SY.dma_start(T.y[:, H:R], T.yo[:, H:R]), "sb", 16)
+        def new_place(k):
+            bt, j, s, P0 = info(k)
+            left = len(wl) - 1 - j
+            m0 = (2 * pk + bt) * M + KB
+            outs = []
+            if s < STEPS - 2 and left:
+                place[bt] = (free[0], place[bt][0])
+                outs.append(T.pos[:, free[0]:free[0] + K])
+                free[0] += K
+            if hops and left < 2:
+                outs.append(T.mo[:, m0 + K * left:m0 + K * (left + 1)])
+            for o in outs:
+                inc(V.tensor_scalar(o, ps[bt][:, 0:K], FLOOR, -FLOOR - 0.5, op.add, op.add), "dx%d" % bt)
+
+        def cells(k):
+            bt = k % 2
+            if k:
+                wait(PE, "dv%d" % (1 - bt))
+            for a, nm in enumerate(("rr", "ww")):
+                wait(PE, nm + str(bt))
+                c0 = 2 * K * bt + K * a
+                for h in range(2):
+                    mm = PE.matmul(T.pso[:, 0:KB], T.mm[:, 128 * (2 * a + h):128 * (2 * a + h + 1)],
+                                   T.rw[:, c0 + h:c0 + K:2], a + h == 0, a + h == 2)
+            inc(mm, "s2%d" % bt)
+
+        def sums(k):
+            bt, j, s, P0 = info(k)
+            if owner != rank:
+                if moves(k):
+                    last = j == len(wl) - 1 or s == STEPS - 2
+                    mm = PE.matmul(ap[bt][:], T.ib[:], T.p[:, P0:P0 + H], j == 0, last)
+                    if last:
+                        inc(mm, "ac%d" % bt)
+                return
+            if not moves(k):
+                wait(PE, "pa%d" % bt)
+                own_add(bt, T.im[:], T.pin, 0)
+                wait(PE, "ga%d" % bt)
+                wait(PE, "gd%d" % bt)
+            own_add(bt, T.ib[:], T.p, P0 - bt * H)
+
+        def new_offsets(k):
+            bt, j, s, P0 = info(k)
+            leaving = j == len(wl) - 1
+            wait(V, "s2%d" % bt)
+            m0 = (2 * pk + bt) * M
+            o0 = (base + j + 1) * K + bt * KB
+            o = T.mo[:, m0:m0 + KB] if leaving else T.off[:, o0:o0 + KB]
+            inc(V.tensor_scalar(o, T.pso[:, 0:KB], -65.0 * (1024 - SHIFT // 16), None, op.add), "dv%d" % bt)
+            if leaving:
+                wait(g, "dx%d" % bt)
+                wait(g, "dv%d" % bt)
+                remote(partner, T.mi[:, m0:m0 + M], T.mo[:, m0:m0 + M], "am%d" % (2 * pk + 2 + bt), hop_mask)
+
+        open_bank(0)
+        for k in range(nh + 2):
+            if moves(k - 2):
+                new_offsets(k - 2)
+            ahead = k == 1 and (pk == 0 or OPT["early1"])
+            if k < nh:
+                gather(A, k)
+            if ahead:
+                gather(V, k)
+            if moves(k - 1):
+                rounds(k - 1)
+            if k < nh and not ahead:
+                gather(V, k)
+            if moves(k - 1):
+                new_place(k - 1)
+                cells(k - 1)
+            if moves(k):
+                slopes(k)
+            if k < nh:
+                sums(k)
+            if moves(k + 1):
+                open_bank(k + 1)
+        if owner != rank and hops:
+            for bt in range(2):
+                wait(V, "ac%d" % bt)
+                inc(V.tensor_scalar(T.po[:, H * bt:H * (bt + 1)], ap[bt][:], -1.0, None, op.mult), "ev%d" % bt)
+                send_sum(bt)
+
+    base = 0
+    for pk in range(len(phases)):
+        run_phase(pk, base)
+        base += len(phases[pk][2])
+
+    outs = ((V, A, "ya", "sa"), (V, SY, "yb", "sb")) if returns else (
+        (A, A, "ya", "sa"), (V, SY, "yb", "sb"), (A, A, "yc", "sa"))
+    for j, (q, st, ev, sem) in enumerate(outs):
+        bank, a, b = own_banks[j]
+        wait(q, "f%d" % j)
+        if returns:
+            wait(V, "pa%d" % j)
+            inc(V.tensor_tensor(T.yo[:, a:b], bank[:], T.pin[:, a:b], op.add), ev)
+        elif q is A:
+            inc(A.activation(T.yo[:, a:b], bank[:, 0:b - a], Copy), ev)
+        else:
+            inc(V.tensor_copy(T.yo[:, a:b], bank[:, 0:b - a]), ev)
+        wait(st, ev)
+        inc(st.dma_start(T.y[:, a:b], T.yo[:, a:b]), sem, 16)
     wait(g, "sent")
     wait(A, "sa")
     wait(SY, "sb")

@@ -9,38 +9,41 @@ KB = K // 2
 BW = 136
 M = KB + 2 * K
 STEPS = 8
+LEAD = 128
+MID = 2048
 FLOOR = 8388607.5
 ROUND1024 = 12884901888.0
 KAPPA = 1.0 / 256
 SHIFT = 512
-OPT = {"kv": 8, "kv0": 16, "kvl": 16, "early1": False, "cut": C}
+OPT = {"end": 192, "kv": 8, "kv0": 16, "kvh": 14, "kvl": 16}
 
 SCRATCH = {
     "w0": ("sbuf", [128, C + 16], "bfloat16"),
     "w1": ("sbuf", [128, C], "bfloat16"),
     "v0": ("sbuf", [128, C + 16], "bfloat16"),
     "v1": ("sbuf", [128, C], "bfloat16"),
+    "sw": ("sbuf", [128, C], "bfloat16"),
+    "st": ("sbuf", [128, C // 8], "bfloat16"),
+    "zero": ("sbuf", [128, C // 8], "bfloat16"),
     "p": ("sbuf", [128, STEPS * R], "bfloat16"),
-    "pxy": ("sbuf", [128, 4 * K], "int32"),
-    "dxy": ("sbuf", [128, 2 * K], "int32"),
-    "fo": ("sbuf", [128, 8], "int32"),
+    "li": ("sbuf", [128, 4 * K + 8], "int32"),
+    "lf": ("sbuf", [128, 4 * K], "float16"),
+    "lc": ("sbuf", [128, 4 * K], "float16"),
     "pi": ("sbuf", [128, 8], "int32"),
     "pm": ("sbuf", [128, 8], "int32"),
     "mk": ("sbuf", [128, 16], "float32"),
     "mb": ("sbuf", [128, 16], "bfloat16"),
     "dg": ("sbuf", [128, BW], "bfloat16"),
+    "dc": ("sbuf", [128, BW], "bfloat16"),
     "band": ("sbuf", [128, 4 * BW], "bfloat16"),
+    "mv": ("sbuf", [128, 3 * BW], "float16"),
     "ib": ("sbuf", [128, 128], "bfloat16"),
     "i2": ("sbuf", [128, 128], "float16"),
     "im": ("sbuf", [128, 128], "float16"),
     "mm": ("sbuf", [128, 4 * 128], "float16"),
     "kap": ("sbuf", [128, K], "bfloat16"),
-    "first": ("sbuf", [128, 8 * K], "float16"),
     "pos": ("sbuf", [128, 32 * K], "float16"),
     "rw": ("sbuf", [128, 4 * K], "float16"),
-    "qx": ("sbuf", [128, K], "float16"),
-    "qy": ("sbuf", [128, K], "int32"),
-    "cs": ("sbuf", [128, K], "float32"),
     "off": ("sbuf", [128, STEPS * K], "uint16"),
     "mo": ("sbuf", [128, 4 * M], "uint16"),
     "mi": ("sbuf", [128, 4 * M], "uint16"),
@@ -57,10 +60,11 @@ SCRATCH = {
     "ap0": ("psum", [128, 512], "float32"),
     "ap1": ("psum", [128, 512], "float32"),
 }
-SEMAPHORES = (["lp", "ld", "lf", "gi", "su", "si", "ep", "sent", "sa", "sb", "fz", "ya", "yb", "yc", "f0", "f1", "f2"]
-              + [a + str(b) for a in ("dv", "dx", "ga", "gd", "mx", "rr", "ww", "s2", "cv", "ac", "ev", "eb", "av", "pa")
+SEMAPHORES = (["lp", "ld", "lq", "gi", "gj", "su", "sv", "sf", "ep", "sent", "sa", "sb", "fz", "f0", "f1", "f2",
+               "zs", "zw", "ls", "as", "lz", "go", "gw", "half"]
+              + [a + str(b) for a in ("dv", "dx", "ga", "gd", "mx", "rr", "ww", "s2", "cv", "ac", "eb", "av", "gl")
                  for b in range(2)]
-              + [a + str(b) for a in ("lw", "am") for b in range(6)])
+              + [a + str(b) for a in ("lw", "am", "pa", "ev", "yy") for b in range(6)])
 
 
 def bits(m):
@@ -79,10 +83,8 @@ def bulk(T, topo, r):
     cores = list(T.cores)
     twin, phases = plan(T, topo, r)
     full = topo.mask(cores[r], cores[twin])
-    spare = full & ~topo.mask(cores[r], cores[(r + 2) % len(cores)])
-    cut = OPT["cut"] if len(phases[0][2]) == 2 else C
-    out = [(0, 0, C // 2, full), (0, C // 2, CF, full), (1, 0, cut, full), (1, cut, C, spare)]
-    return [x for x in out if x[1] < x[2]]
+    mid = MID if len(phases[0][2]) == 4 else C // 2
+    return [(0, 0, LEAD, full), (0, LEAD, CF, full), (1, 0, mid, full), (1, mid, C, full)]
 
 
 def rank_program(g, core, T, topo):
@@ -109,114 +111,203 @@ def rank_program(g, core, T, topo):
     def wait(q, name):
         q.wait_ge(S[name], cnt[name])
 
-    def remote(to, out_ap, in_ap, rsem, mask):
+    def remote(to, out_ap, in_ap, rsem, mask, lsem="sent"):
         rid, pid, _se = topo.addr(to)
-        g.remote_dma(out_ap, in_ap, S[rsem], S.sent, pid, rid, mask)
-        cnt["sent"] += bits(mask)
+        g.remote_dma(out_ap, in_ap, S[rsem], S[lsem], pid, rid, mask)
+        cnt[lsem] = cnt.get(lsem, 0) + bits(mask)
+
+    parts = [(0, H), (H, R - OPT["end"]), (R - OPT["end"], R)] if returns else [(0, H), (H, R)]
 
     for (l, a, b, m) in bulk(T, topo, twin):
         cnt["av%d" % l] = cnt.get("av%d" % l, 0) + bits(m)
-    for bt in range(2):
-        cnt["pa%d" % bt] = bits(topo.mask(partner, core))
-        for k in range(1, len(phases)):
-            cnt["am%d" % (2 * k + bt)] = bits(topo.mask(partner, core))
+    for j in range(len(parts)):
+        cnt["pa%d" % j] = bits(topo.mask(partner, core))
+    for k in range(2, 2 * len(phases)):
+        cnt["am%d" % k] = bits(topo.mask(partner, core))
 
-    inc(SY.dma_start(T.pxy[:, 0:K], T.px[:]), "lp", 16)
-    inc(A.dma_start(T.pxy[:, K:2 * K], T.py[:]), "lp", 16)
-    inc(A.dma_start(T.fo[:, 0:2], T.fac[:]), "lf", 16)
-    inc(SY.dma_start(T.dxy[:, 0:K], T.dx[:]), "ld", 16)
-    inc(A.dma_start(T.dxy[:, K:2 * K], T.dy[:]), "ld", 16)
-    for k, (l, a, b, m) in enumerate(pieces):
-        b = min(b, C)
-        inc(SY.dma_start((T.w0, T.w1)[l][:, a:b], T.lay[:, C * l + a:C * l + b]), "lw%d" % k, 16)
-    arrive = {l: ["lw%d" % k for k, x in enumerate(pieces) if x[0] == l] for l in range(2)}
-    arrive.update({2: ["av0"], 3: ["av1"]})
+    inc(SY.dma_start(T.w0[:, 0:LEAD], T.lay[:, 0:LEAD]), "lw2", 16)
+    for k, (q, t) in enumerate(((A, T.px), (SY, T.py), (SY, T.dx), (A, T.dy))):
+        inc(q.dma_start(T.li[32 * k:32 * (k + 1), 0:4 * K], t[:]), "lp" if k < 2 else "ld", 16)
+        if k == 1:
+            inc(A.dma_start(T.li[:, 4 * K:4 * K + 2], T.fac[:]), "lq", 16)
+    inc(SY.dma_start(T.w0[:, LEAD:C], T.lay[:, LEAD:C]), "lw0", 16)
+    second = [x for x in pieces if x[0] == 1]
+    arrive = [["lw0", "lw2"], ["lw1"] if returns else ["lw1", "lw3"], ["av0"], ["av1"], ["lz"]]
+
+    def load_second():
+        for (l, a, b, m), nm in zip([(1, 0, C, 0)] if returns else second, arrive[1]):
+            inc(SY.dma_start(T.w1[:, a:b], T.lay[:, C + a:C + b]), nm, 16)
+
+    chunk = C // 8
+    inc(V.memset(T.zero[:], 0.0), "zs")
+    wait(A, "zs")
+    vz = 3 if returns else 2
+    for c in range(vz, 8):
+        inc(A.activation(T.sw[:, chunk * c:chunk * (c + 1)], T.zero[:], Copy), "zw")
+    if returns:
+        load_second()
+        cnt["as"] = bits(topo.mask(cores[twin], core))
+        wait(SY, "as")
+    else:
+        for a in range(2):
+            inc(SY.dma_start(T.st[64 * a:64 * (a + 1), :], T.lay[14 + a:128:16, C:2 * C]), "ls", 16)
+    early = 3 if returns else 1
 
     inc(g.iota(T.pi[:, 0:1], [[1, 1]], 0, 1), "gi")
     wait(V, "gi")
+    inc(g.iota(T.dc[:], [[1, BW]], 0, 0, allow_small_or_imprecise_dtypes=True), "gj")
     inc(g.iota(T.dg[:], [[1, BW]], 0, -1, allow_small_or_imprecise_dtypes=True), "gi")
-    inc(V.tensor_scalar(T.pm[:, 0:1], T.pi[:, 0:1], 15, None, op.bitwise_and), "su")
-    inc(V.memset(T.kap[:], KAPPA), "su")
-    wait(V, "su")
     col = {}
-    for k, (nm, s1, s2, o0, o1) in enumerate((
-            ("slope", 14.0, 1.0 / 128, op.is_ge, op.mult),
-            ("diag", 7.0, -105.0, op.mult, op.add),
-            ("down", 8.0, -8.0, op.is_ge, op.mult),
-            ("up", 8.0, 8.0, op.is_lt, op.mult),
-            ("low", 8.0, 1.0, op.is_lt, op.mult),
-            ("high", 8.0, 1.0 / 64, op.is_ge, op.mult),
-            ("h63", 8.0, 63.0, op.is_ge, op.mult))):
-        col[nm] = (T.mb if nm == "diag" else T.mk)[:, k:k + 1]
-        inc(V.tensor_scalar(col[nm], T.pm[:, 0:1], s1, s2, o0, o1), "su")
-    wait(V, "gi")
-    for buf, val in ((T.ib, 1.0), (T.i2, 2.0), (T.im, -1.0)):
-        inc(V.tensor_scalar(buf[:], T.dg[:, 0:128], 0.0, val, op.is_equal, op.mult), "su")
-    wait(V, "su")
-    col["wr"], col["ww"] = T.mk[:, 8:9], T.mk[:, 9:10]
-    inc(V.tensor_scalar(col["wr"], col["h63"], 1.0, None, op.add), "su")
-    inc(V.tensor_scalar(col["ww"], col["h63"], 1.0, -1.0 / 16, op.add, op.mult), "su")
-    wait(V, "su")
-    for k, (d, w) in enumerate((("down", "wr"), ("up", "wr"), ("down", "ww"), ("up", "ww"))):
-        inc(V.tensor_scalar(T.mm[:, 128 * k:128 * (k + 1)], T.dg[:, 0:128], col[d], col[w], op.is_equal, op.mult), "su")
 
-    wait(V, "lp")
-    inc(V.tensor_scalar(T.qx[:], T.pxy[:, 0:K], 1.0 / 64, 256.0 - 15.0 / 128, op.mult, op.add), "si")
-    inc(V.tensor_scalar(T.qy[:], T.pxy[:, K:2 * K], 1008, None, op.bitwise_and), "si")
-    wait(V, "lf")
-    inc(V.tensor_scalar(T.w0[:, C:CF], T.fo[:, 0:2], col["slope"], None, op.mult), "fz")
-    wait(V, "si")
-    inc(V.tensor_tensor(T.cs[:], T.qy[:], T.qx[:], op.add), "si")
-    wait(V, "ld")
-    inc(V.tensor_tensor(T.pxy[:, 2 * K:4 * K], T.pxy[:, 0:2 * K], T.dxy[:], op.subtract), "su")
-    wait(V, "si")
-    inc(V.tensor_scalar(T.off[:, 0:K], T.cs[:], 4.0, -1024.0, op.mult, op.add), "dv0")
+    def column(nm, src, s1, s2, o0, o1):
+        col[nm] = (T.mb if nm == "diag" else T.mk)[:, len(col):len(col) + 1]
+        inc(V.tensor_scalar(col[nm], src, s1, s2, o0, o1), "su")
+
+    def band(o, src, at, weight):
+        inc(V.tensor_scalar(o, src, at, weight, op.is_equal, op.mult), "su")
+
+    p31, p32, p29, p2, p15 = [T.pm[:, k:k + 1] for k in range(5)]
+    for o, m in ((p31, 31), (p32, 32), (p29, 29), (p2, 2), (p15, 15)):
+        inc(V.tensor_scalar(o, T.pi[:, 0:1], m, None, op.bitwise_and), "su")
+    column("shift", T.pi[:, 0:1], 64.0, float(SHIFT), op.is_lt, op.mult)
     wait(V, "su")
-    for h, nm in enumerate(("low", "high")):
-        inc(V.tensor_scalar(T.first[:, 4 * K * h:4 * K * (h + 1)], T.pxy[:], float(SHIFT), col[nm], op.add, op.mult), "su")
-    wait(V, "fz")
+    column("row", p31, 4.0, 3.0, op.mult, op.add)
+    column("xy", p32, 63.0 / 32, 1.0, op.mult, op.add)
+    column("t1", p29, 4.0, 3.0, op.mult, op.add)
+    column("h0", p2, 0.0, 1.0, op.is_equal, op.mult)
+    column("h1", p2, 2.0, 1.0, op.is_equal, op.mult)
+    column("h63", p15, 8.0, 63.0, op.is_ge, op.mult)
+    column("slope", p15, 14.0, 1.0 / 128, op.is_ge, op.mult)
+    column("diag", p15, 7.0, -105.0, op.mult, op.add)
+    wait(V, "su")
+    wait(V, "gj")
+    band(T.mv[:, 2 * BW:3 * BW], T.dc[:], col["row"], col["xy"])
+    wait(PE, "su")
+    column("to", p32, 0.25, col["t1"], op.mult, op.add)
+    column("wr", col["h63"], 1.0, 1.0, op.add, op.mult)
+    column("ww", col["h63"], 1.0, -1.0 / 16, op.add, op.mult)
+    column("down", p15, 8.0, -8.0, op.is_ge, op.mult)
+    column("up", p15, 8.0, 8.0, op.is_lt, op.mult)
+    inc(V.memset(T.kap[:], KAPPA), "su")
+    wait(V, "gi")
+    band(T.ib[:], T.dg[:, 0:128], 0.0, 1.0)
+    wait(V, "lp")
+    inc(V.tensor_scalar(T.lc[0:64, :], T.li[0:64, 0:4 * K], 1.0 / 16, 1055.5 + 1.0 / 32, op.mult, op.add), "sv")
+    wait(V, "su")
+    for h in range(2):
+        band(T.mv[:, BW * h:BW * (h + 1)], T.dc[:], col["to"], col["h%d" % h])
+    wait(V, "lq")
+    inc(V.tensor_scalar(T.w0[:, C:CF], T.li[:, 4 * K:4 * K + 2], col["slope"], None, op.mult), "fz")
+    wait(V, "ld")
+    inc(V.tensor_scalar(T.lf[:], T.li[:, 0:4 * K], col["shift"], None, op.add), "sf")
+
+    wins = (T.w0, T.w1, T.v0, T.v1, T.sw)
+    ps = (T.ps0, T.ps1)
+    ap = (T.ap0, T.ap1)
+    place = {}
+    free = [0]
+    seen = {}
+
+    def once(key):
+        new = key not in seen
+        seen[key] = 1
+        return new
+
+    def spread(bank, bt, rows, stop):
+        for h in range(2):
+            for j in range(4):
+                mm = PE.matmul(bank[:, h:K:2], T.mv[0:rows, BW * h + 3 - j:BW * h + 131 - j],
+                               T.lf[0:rows, K * j + KB * bt:K * j + KB * (bt + 1)], False, stop and h + j == 4)
+        return mm
+
+    def rounds(bt):
+        wait(V, "mx%d" % bt)
+        inc(V.tensor_scalar(T.rw[:, 2 * K * bt:2 * K * bt + K], ps[bt][:, 0:K], 1.0 / 16, 1023.5, op.mult, op.add),
+            "rr%d" % bt)
+        inc(V.tensor_scalar(T.rw[:, 2 * K * bt + K:2 * K * (bt + 1)], ps[bt][:, 0:K], ROUND1024, -ROUND1024,
+                            op.add, op.add), "ww%d" % bt)
+
+    def whole_place(o, bank, sem):
+        inc(V.tensor_scalar(o, bank[:, 0:K], FLOOR, -FLOOR - 0.5, op.add, op.add), sem)
+
+    def keep_place(bt, bank, sem):
+        place[bt] = (free[0], place.get(bt, (None,))[0])
+        whole_place(T.pos[:, free[0]:free[0] + K], bank, sem)
+        free[0] += K
+
+    def cells(bt):
+        if once("cells"):
+            wait(PE, "su")
+            wait(PE, "dv0")
+        if "dv%d" % (1 - bt) in cnt:
+            wait(PE, "dv%d" % (1 - bt))
+        for a, nm in enumerate(("rr", "ww")):
+            wait(PE, nm + str(bt))
+            c0 = 2 * K * bt + K * a
+            for h in range(2):
+                mm = PE.matmul(T.pso[:, 0:KB], T.mm[:, 128 * (2 * a + h):128 * (2 * a + h + 1)],
+                               T.rw[:, c0 + h:c0 + K:2], a + h == 0, a + h == 2)
+        inc(mm, "s2%d" % bt)
+
+    def offsets(bt, o):
+        wait(V, "s2%d" % bt)
+        inc(V.tensor_scalar(o, T.pso[:, 0:KB], -65.0 * (1024 - SHIFT // 16), None, op.add), "dv%d" % bt)
 
     def make_bands(l0, w):
         for l in range(2):
             inc(V.tensor_scalar(T.band[:, BW * (l0 + l):BW * (l0 + l + 1)], T.dg[:], col["diag"], w[:, C + l:C + l + 1],
                                 op.is_equal, op.mult), "ep")
 
-    make_bands(0, T.w0)
+    wait(PE, "sv")
+    for j in range(4):
+        mm = PE.matmul(T.pso[:, 0:K], T.mv[0:64, 2 * BW + 3 - j:2 * BW + 131 - j], T.lc[0:64, K * j:K * (j + 1)],
+                       j == 0, j == 3)
+    inc(mm, "sv")
+    wait(V, "sv")
+    inc(V.tensor_scalar(T.off[:, 0:K], T.pso[:, 0:K], -65.0 * 1056, None, op.add), "dv0")
     wait(PE, "su")
-    for h in range(2):
-        for k in range(2):
-            o = T.pso[:, 2 * K * h + K * k:2 * K * h + K * (k + 1)]
-            c0 = 4 * K * h + 2 * K * k
-            PE.matmul(o, T.mm[:, 0:128], T.first[:, c0:c0 + K], True, False)
-            mm = PE.matmul(o, T.mm[:, 128:256], T.first[:, c0 + K:c0 + 2 * K], False, True)
-    inc(mm, "si")
-    wait(V, "si")
-    for h in range(2):
-        inc(V.tensor_copy(T.pos[:, h:4 * K:2], T.pso[:, 2 * K * h:2 * K * (h + 1)]), "dx0")
+    wait(PE, "sf")
+    wait(V, "fz")
+    make_bands(0, T.w0)
+    if not returns:
+        inc(V.memset(T.sw[:, 0:chunk * vz], 0.0), "zw")
+    for k, (d, w) in enumerate((("down", "wr"), ("up", "wr"), ("down", "ww"), ("up", "ww"))):
+        band(T.mm[:, 128 * k:128 * (k + 1)], T.dg[:, 0:128], col[d], col[w])
 
-    for k, (l, a, b, m) in enumerate(pieces):
-        wait(g, "lw%d" % k)
+    def place_slopes():
+        wait(SY, "zw")
+        for a in range(2):
+            src = T.st[64 * a:64 * (a + 1), :] if returns else T.lay[14 + a:128:16, C:2 * C]
+            inc(SY.dma_start(T.sw[14 + a:128:16, :], src), "lz", 16)
+        SY.sem_inc(S.go, 1)
+
+    if not returns:
+        place_slopes()
+
+    def send_piece(l, a, b, m):
+        wait(g, "lw2" if b == LEAD else arrive[1][-1] if l and a else "lw%d" % l)
         if b > C:
             wait(g, "fz")
-        remote(cores[twin], (T.v0, T.v1)[l][:, a:b], (T.w0, T.w1)[l][:, a:b], "av%d" % l, m)
+        if (l, a) == ((1, MID) if returns else (0, LEAD)):
+            g.wait_ge(S.go, 1)
+            if returns:
+                wait(g, "half")
+        remote(cores[twin], (T.v0, T.v1)[l][:, a:b], (T.w0, T.w1)[l][:, a:b], "av%d" % l, m,
+               "half" if returns and (l, a) == (1, 0) else "sent")
 
-    wins = (T.w0, T.w1, T.v0, T.v1)
-    ps = (T.ps0, T.ps1)
-    ap = (T.ap0, T.ap1)
-    place = {0: (0, 2 * K), 1: (K, 3 * K)}
-    free = [4 * K]
-    seen = {}
+    for x in pieces:
+        if x[0] == 0 or returns:
+            send_piece(*x)
+    if not returns:
+        wait(g, "ls")
+        remote(cores[twin], T.st[:], T.st[:], "as", topo.mask(core, cores[twin]))
+
     if returns:
         own_banks = [(T.ao0, 0, H), (T.ao1, H, R)]
     else:
         own_banks = [(T.ao0, 0, H), (T.ao1, H, H + H // 2), (T.ao2, H + H // 2, R)]
     own_all = sum(len(w) for (o, s0, w) in phases if o == rank) + int(not returns)
     own_done = {0: 0, 1: 0}
-
-    def once(key):
-        new = key not in seen
-        seen[key] = 1
-        return new
 
     def own_add(bt, lhs, buf, c0):
         own_done[bt] += 1
@@ -226,9 +317,19 @@ def rank_program(g, core, T, topo):
                 if own_done[bt] == own_all:
                     inc(mm, "f%d" % j)
 
-    def send_sum(bt):
-        wait(g, "ev%d" % bt)
-        remote(partner, T.pin[:, H * bt:H * (bt + 1)], T.po[:, H * bt:H * (bt + 1)], "pa%d" % bt, hop_mask)
+    def late_gathers():
+        for nm in arrive[early]:
+            wait(A, nm)
+        for bt in range(2):
+            P0, o0 = early * R + bt * H, early * K + bt * KB
+            inc(A.activation(T.p[:, P0:P0 + H], wins[early][:, 0:C].indirect(T.off[:, o0:o0 + KB]), Copy), "gl%d" % bt)
+            wait(PE, "gl%d" % bt)
+            own_add(bt, T.ib[:], T.p, early * R)
+
+    def send_sum(j):
+        a, b = parts[j]
+        wait(g, "ev%d" % j)
+        remote(partner, T.pin[:, a:b], T.po[:, a:b], "pa%d" % j, hop_mask)
 
     def run_phase(pk, base):
         owner, s0, wl = phases[pk]
@@ -247,9 +348,9 @@ def rank_program(g, core, T, topo):
 
         def share(k):
             if k == 0:
-                return OPT["kv0"]
+                return OPT["kvh"] if pk else OPT["kv0"]
             if not moves(k):
-                return KB if owner != rank else OPT["kvl"] if k % 2 else OPT["kv"]
+                return KB if returns else OPT["kvl"] if k % 2 else OPT["kv"]
             return OPT["kv"]
 
         def gather(q, k):
@@ -259,34 +360,40 @@ def rank_program(g, core, T, topo):
             else:
                 buf, o0, sem = T.off, (base + j) * K + bt * KB, "dv%d" % (bt if s else 0)
             ka = KB - share(k)
-            half = slice(H * bt, H * (bt + 1))
             if q is A and not ka:
                 wait(A, "ac%d" % bt)
-                inc(A.activation(T.se[:, half], ap[bt][:], Copy), "eb%d" % bt)
+                inc(A.activation(T.se[:, H * bt:H * (bt + 1)], ap[bt][:], Copy), "eb%d" % bt)
                 return
             wait(q, sem)
-            for nm in arrive[wl[j]]:
-                if once((nm, q is A)):
+            w = 4 if pk == 0 and s == early else wl[j]
+            if once((w, q is A)):
+                for nm in arrive[w]:
                     wait(q, nm)
-            win = wins[wl[j]][:, 0:C]
+            win = wins[w][:, 0:C]
             if q is A:
                 inc(A.activation(T.p[:, P0:P0 + 16 * ka], win.indirect(buf[:, o0:o0 + ka]), Copy), "ga%d" % bt)
             elif not ka:
                 wait(V, "eb%d" % bt)
-                inc(V.tensor_tensor(T.po[:, half], win.indirect(buf[:, o0:o0 + KB]), T.se[:, half], op.add), "ev%d" % bt)
-                send_sum(bt)
+                for jp, (a, b) in enumerate(parts):
+                    if a // H == bt:
+                        c0 = o0 + (a - H * bt) // 16
+                        inc(V.tensor_tensor(T.po[:, a:b], win.indirect(buf[:, c0:c0 + (b - a) // 16]), T.se[:, a:b],
+                                            op.add), "ev%d" % jp)
+                        send_sum(jp)
             else:
-                inc(V.tensor_copy(T.p[:, P0 + 16 * ka:P0 + H], win.indirect(buf[:, o0 + ka:o0 + KB])), "gd%d" % bt)
+                if wl[j] == 2 and once("bands"):
+                    make_bands(2, T.v0)
                 if landed(k):
                     c0 = free[0]
                     free[0] += 2 * K
                     place[bt] = (c0, c0 + K)
                     inc(V.tensor_copy(T.pos[:, c0:c0 + 2 * K], buf[:, o0 + KB:o0 + M]), "cv%d" % bt)
-                if wl[j] == 2 and once("bands"):
-                    make_bands(2, T.v0)
+                inc(V.tensor_copy(T.p[:, P0 + 16 * ka:P0 + H], win.indirect(buf[:, o0 + ka:o0 + KB])), "gd%d" % bt)
 
         def positions(k, stop):
             bt = k % 2
+            if once("twice"):
+                wait(PE, "su")
             a, b = place[bt]
             PE.matmul(ps[bt][:, 0:K], T.i2[:], T.pos[:, a:a + K], False, False)
             return PE.matmul(ps[bt][:, 0:K], T.im[:], T.pos[:, b:b + K], False, stop)
@@ -296,57 +403,33 @@ def rank_program(g, core, T, topo):
             if "dx%d" % bt in cnt:
                 wait(PE, "dx%d" % bt)
             PE.matmul(ps[bt][:, 0:K], T.ib[:], T.kap[:], True, False)
-            if not landed(k):
+            if pk == 0 and k < 2:
+                spread(ps[bt], bt, 128, False)
+            elif not landed(k):
                 positions(k, False)
 
         def slopes(k):
             bt, j, s, P0 = info(k)
             if once(("band", wl[j] // 2)):
                 wait(PE, "ep")
+            if landed(k):
+                wait(PE, "cv%d" % bt)
+                positions(k, False)
             wait(PE, "ga%d" % bt)
             wait(PE, "gd%d" % bt)
             b0 = BW * wl[j] + 7
             for i in range(8):
-                mm = PE.matmul(ps[bt][:, 0:K], T.band[:, b0 - i:b0 - i + 128], T.p[:, P0 + i:P0 + H:8], False,
-                               i == 7 and not landed(k))
-            if landed(k):
-                wait(PE, "cv%d" % bt)
-                mm = positions(k, True)
+                mm = PE.matmul(ps[bt][:, 0:K], T.band[:, b0 - i:b0 - i + 128], T.p[:, P0 + i:P0 + H:8], False, i == 7)
             inc(mm, "mx%d" % bt)
-
-        def rounds(k):
-            bt = k % 2
-            wait(V, "mx%d" % bt)
-            inc(V.tensor_scalar(T.rw[:, 2 * K * bt:2 * K * bt + K], ps[bt][:, 0:K], 1.0 / 16, 1023.5, op.mult, op.add),
-                "rr%d" % bt)
-            inc(V.tensor_scalar(T.rw[:, 2 * K * bt + K:2 * K * (bt + 1)], ps[bt][:, 0:K], ROUND1024, -ROUND1024,
-                                op.add, op.add), "ww%d" % bt)
 
         def new_place(k):
             bt, j, s, P0 = info(k)
             left = len(wl) - 1 - j
             m0 = (2 * pk + bt) * M + KB
-            outs = []
             if s < STEPS - 2 and left:
-                place[bt] = (free[0], place[bt][0])
-                outs.append(T.pos[:, free[0]:free[0] + K])
-                free[0] += K
+                keep_place(bt, ps[bt], "dx%d" % bt)
             if hops and left < 2:
-                outs.append(T.mo[:, m0 + K * left:m0 + K * (left + 1)])
-            for o in outs:
-                inc(V.tensor_scalar(o, ps[bt][:, 0:K], FLOOR, -FLOOR - 0.5, op.add, op.add), "dx%d" % bt)
-
-        def cells(k):
-            bt = k % 2
-            if k:
-                wait(PE, "dv%d" % (1 - bt))
-            for a, nm in enumerate(("rr", "ww")):
-                wait(PE, nm + str(bt))
-                c0 = 2 * K * bt + K * a
-                for h in range(2):
-                    mm = PE.matmul(T.pso[:, 0:KB], T.mm[:, 128 * (2 * a + h):128 * (2 * a + h + 1)],
-                                   T.rw[:, c0 + h:c0 + K:2], a + h == 0, a + h == 2)
-            inc(mm, "s2%d" % bt)
+                whole_place(T.mo[:, m0 + K * left:m0 + K * (left + 1)], ps[bt], "dx%d" % bt)
 
         def sums(k):
             bt, j, s, P0 = info(k)
@@ -357,6 +440,8 @@ def rank_program(g, core, T, topo):
                     if last:
                         inc(mm, "ac%d" % bt)
                 return
+            if s == early:
+                return
             if not moves(k):
                 wait(PE, "pa%d" % bt)
                 own_add(bt, T.im[:], T.pin, 0)
@@ -366,39 +451,64 @@ def rank_program(g, core, T, topo):
 
         def new_offsets(k):
             bt, j, s, P0 = info(k)
-            leaving = j == len(wl) - 1
-            wait(V, "s2%d" % bt)
             m0 = (2 * pk + bt) * M
             o0 = (base + j + 1) * K + bt * KB
-            o = T.mo[:, m0:m0 + KB] if leaving else T.off[:, o0:o0 + KB]
-            inc(V.tensor_scalar(o, T.pso[:, 0:KB], -65.0 * (1024 - SHIFT // 16), None, op.add), "dv%d" % bt)
-            if leaving:
-                wait(g, "dx%d" % bt)
-                wait(g, "dv%d" % bt)
-                remote(partner, T.mi[:, m0:m0 + M], T.mo[:, m0:m0 + M], "am%d" % (2 * pk + 2 + bt), hop_mask)
+            if j < len(wl) - 1:
+                offsets(bt, T.off[:, o0:o0 + KB])
+                return
+            offsets(bt, T.mo[:, m0:m0 + KB])
+            wait(g, "dx%d" % bt)
+            wait(g, "dv%d" % bt)
+            remote(partner, T.mi[:, m0:m0 + M], T.mo[:, m0:m0 + M], "am%d" % (2 * pk + 2 + bt), hop_mask)
+            if pk == 0 and bt == 1 and not returns:
+                g.sem_inc(S.gw, 1)
+                SY.wait_ge(S.gw, 1)
+                load_second()
+                for x in second:
+                    send_piece(*x)
 
         open_bank(0)
+        if pk == 0:
+            open_bank(1)
+            for bt in range(2):
+                PE.matmul(ap[bt][:, 0:K], T.ib[:], T.kap[:], True, False)
+                mm = spread(ap[bt], bt, 64, True)
+            inc(mm, "sf")
         for k in range(nh + 2):
             if moves(k - 2):
                 new_offsets(k - 2)
-            ahead = k == 1 and (pk == 0 or OPT["early1"])
+            ahead = k == 1 and pk == 0
             if k < nh:
                 gather(A, k)
             if ahead:
                 gather(V, k)
+                wait(V, "sf")
+                for bt in range(2):
+                    keep_place(bt, ap[bt], "su")
+                for buf, val in ((T.i2, 2.0), (T.im, -1.0)):
+                    band(buf[:], T.dg[:, 0:128], 0.0, val)
+            if pk == 0 and returns and 2 <= k <= vz + 1:
+                inc(V.memset(T.sw[:, chunk * (k - 2):chunk * (k - 1)], 0.0), "zw")
+                if k == vz + 1:
+                    place_slopes()
             if moves(k - 1):
-                rounds(k - 1)
+                rounds((k - 1) % 2)
             if k < nh and not ahead:
                 gather(V, k)
             if moves(k - 1):
                 new_place(k - 1)
-                cells(k - 1)
+                cells((k - 1) % 2)
             if moves(k):
                 slopes(k)
             if k < nh:
                 sums(k)
-            if moves(k + 1):
+            if moves(k + 1) and (pk or k):
                 open_bank(k + 1)
+        if pk == 0 and once("bands"):
+            wait(V, "av0")
+            make_bands(2, T.v0)
+        if pk == 1:
+            late_gathers()
         if owner != rank and hops:
             for bt in range(2):
                 wait(V, "ac%d" % bt)
@@ -410,18 +520,20 @@ def rank_program(g, core, T, topo):
         run_phase(pk, base)
         base += len(phases[pk][2])
 
-    outs = ((V, A, "ya", "sa"), (V, SY, "yb", "sb")) if returns else (
-        (A, A, "ya", "sa"), (V, SY, "yb", "sb"), (A, A, "yc", "sa"))
-    for j, (q, st, ev, sem) in enumerate(outs):
-        bank, a, b = own_banks[j]
-        wait(q, "f%d" % j)
+    for j, (a, b) in enumerate(parts if returns else [x[1:] for x in own_banks]):
+        st, sem = ((A, "sa"), (SY, "sb"))[j % 2]
+        ev = "yy%d" % j
         if returns:
+            bt = a // H
+            wait(V, "f%d" % bt)
             wait(V, "pa%d" % j)
-            inc(V.tensor_tensor(T.yo[:, a:b], bank[:], T.pin[:, a:b], op.add), ev)
-        elif q is A:
-            inc(A.activation(T.yo[:, a:b], bank[:, 0:b - a], Copy), ev)
+            inc(V.tensor_tensor(T.yo[:, a:b], own_banks[bt][0][:, a - H * bt:b - H * bt], T.pin[:, a:b], op.add), ev)
+        elif st is A:
+            wait(A, "f%d" % j)
+            inc(A.activation(T.yo[:, a:b], own_banks[j][0][:, 0:b - a], Copy), ev)
         else:
-            inc(V.tensor_copy(T.yo[:, a:b], bank[:, 0:b - a]), ev)
+            wait(V, "f%d" % j)
+            inc(V.tensor_copy(T.yo[:, a:b], own_banks[j][0][:, 0:b - a]), ev)
         wait(st, ev)
         inc(st.dma_start(T.y[:, a:b], T.yo[:, a:b]), sem, 16)
     wait(g, "sent")

from concourse.mybir import AluOpType, ActivationFunctionType

C = 4096
CF = C + 2
R = 1024
H = R // 2
K = R // 16
KB = K // 2
BW = 136
M = KB + 2 * K
STEPS = 8
LEAD = 128
MID = 2048
FLOOR = 8388607.5
ROUND1024 = 12884901888.0
KAPPA = 1.0 / 256
SHIFT = 512
OPT = {"end": 192, "kv": 8, "kv0": 16, "kvh": 14, "kvl": 16}

SCRATCH = {
    "w0": ("sbuf", [128, C + 16], "bfloat16"),
    "w1": ("sbuf", [128, C], "bfloat16"),
    "v0": ("sbuf", [128, C + 16], "bfloat16"),
    "v1": ("sbuf", [128, C], "bfloat16"),
    "sw": ("sbuf", [128, C], "bfloat16"),
    "st": ("sbuf", [128, C // 8], "bfloat16"),
    "zero": ("sbuf", [128, C // 8], "bfloat16"),
    "p": ("sbuf", [128, STEPS * R], "bfloat16"),
    "li": ("sbuf", [128, 4 * K + 8], "int32"),
    "lf": ("sbuf", [128, 4 * K], "float16"),
    "lc": ("sbuf", [128, 4 * K], "float16"),
    "pi": ("sbuf", [128, 8], "int32"),
    "pm": ("sbuf", [128, 8], "int32"),
    "mk": ("sbuf", [128, 16], "float32"),
    "mb": ("sbuf", [128, 16], "bfloat16"),
    "dg": ("sbuf", [128, BW], "bfloat16"),
    "dc": ("sbuf", [128, BW], "bfloat16"),
    "band": ("sbuf", [128, 4 * BW], "bfloat16"),
    "mv": ("sbuf", [128, 3 * BW], "float16"),
    "ib": ("sbuf", [128, 128], "bfloat16"),
    "i2": ("sbuf", [128, 128], "float16"),
    "im": ("sbuf", [128, 128], "float16"),
    "mm": ("sbuf", [128, 4 * 128], "float16"),
    "kap": ("sbuf", [128, K], "bfloat16"),
    "pos": ("sbuf", [128, 32 * K], "float16"),
    "rw": ("sbuf", [128, 4 * K], "float16"),
    "off": ("sbuf", [128, STEPS * K], "uint16"),
    "mo": ("sbuf", [128, 4 * M], "uint16"),
    "mi": ("sbuf", [128, 4 * M], "uint16"),
    "po": ("sbuf", [128, R], "float16"),
    "pin": ("sbuf", [128, R], "float16"),
    "yo": ("sbuf", [128, R], "float32"),
    "se": ("sbuf", [128, R], "float32"),
    "ps0": ("psum", [128, 512], "float32"),
    "ps1": ("psum", [128, 512], "float32"),
    "pso": ("psum", [128, 512], "float32"),
    "ao0": ("psum", [128, 512], "float32"),
    "ao1": ("psum", [128, 512], "float32"),
    "ao2": ("psum", [128, 512], "float32"),
    "ap0": ("psum", [128, 512], "float32"),
    "ap1": ("psum", [128, 512], "float32"),
}
SEMAPHORES = (["lp", "ld", "lq", "gi", "gj", "su", "sv", "sf", "ep", "sent", "sa", "sb", "fz", "f0", "f1", "f2",
               "zs", "zw", "ls", "as", "lz", "go", "gw", "half"]
              + [a + str(b) for a in ("dv", "dx", "ga", "gd", "mx", "rr", "ww", "s2", "cv", "ac", "eb", "av", "gl")
                 for b in range(2)]
              + [a + str(b) for a in ("lw", "am", "pa", "ev", "yy") for b in range(6)])


def bits(m):
    return bin(m).count("1")


def plan(T, topo, r):
    cores = list(T.cores)
    n = len(cores)
    if topo.chip(cores[r]) == topo.chip(cores[(r + 1) % n]):
        return (r + 1) % n, [(r, 0, [0, 1, 2, 3]), ((r + 2) % n, 4, [0, 1, 2, 3])]
    return (r - 1) % n, [(r, 0, [0, 1]), ((r + 2) % n, 2, [2, 3, 0, 1]), (r, 6, [2, 3])]


def bulk(T, topo, r):
    cores = list(T.cores)
    twin, phases = plan(T, topo, r)
    full = topo.mask(cores[r], cores[twin])
    mid = MID if len(phases[0][2]) == 4 else C // 2
    return [(0, 0, LEAD, full), (0, LEAD, CF, full), (1, 0, mid, full), (1, mid, C, full)]


def rank_program(g, core, T, topo):
    rank = T.rank_of(core)
    if rank is None:
        return
    cores = list(T.cores)
    n = len(cores)
    S = T.sem
    V, A, PE, SY = g.vector, g.scalar, g.tensor, g.sync
    op = AluOpType
    Copy = ActivationFunctionType.Copy
    twin, phases = plan(T, topo, rank)
    pieces = bulk(T, topo, rank)
    partner = cores[(rank + 2) % n]
    hop_mask = topo.mask(core, partner)
    returns = phases[-1][0] != rank
    cnt = {"sent": 0}

    def inc(ins, name, k=1):
        ins.then_inc(S[name], k)
        cnt[name] = cnt.get(name, 0) + k

    def wait(q, name):
        q.wait_ge(S[name], cnt[name])

    def remote(to, out_ap, in_ap, rsem, mask, lsem="sent"):
        rid, pid, _se = topo.addr(to)
        g.remote_dma(out_ap, in_ap, S[rsem], S[lsem], pid, rid, mask)
        cnt[lsem] = cnt.get(lsem, 0) + bits(mask)

    parts = [(0, H), (H, R - OPT["end"]), (R - OPT["end"], R)] if returns else [(0, H), (H, R)]

    for (l, a, b, m) in bulk(T, topo, twin):
        cnt["av%d" % l] = cnt.get("av%d" % l, 0) + bits(m)
    for j in range(len(parts)):
        cnt["pa%d" % j] = bits(topo.mask(partner, core))
    for k in range(2, 2 * len(phases)):
        cnt["am%d" % k] = bits(topo.mask(partner, core))

    inc(SY.dma_start(T.w0[:, 0:LEAD], T.lay[:, 0:LEAD]), "lw2", 16)
    for k, (q, t) in enumerate(((A, T.px), (SY, T.py), (SY, T.dx), (A, T.dy))):
        inc(q.dma_start(T.li[32 * k:32 * (k + 1), 0:4 * K], t[:]), "lp" if k < 2 else "ld", 16)
        if k == 1:
            inc(A.dma_start(T.li[:, 4 * K:4 * K + 2], T.fac[:]), "lq", 16)
    inc(SY.dma_start(T.w0[:, LEAD:C], T.lay[:, LEAD:C]), "lw0", 16)
    second = [x for x in pieces if x[0] == 1]
    arrive = [["lw0", "lw2"], ["lw1"] if returns else ["lw1", "lw3"], ["av0"], ["av1"], ["lz"]]

    def load_second():
        for (l, a, b, m), nm in zip([(1, 0, C, 0)] if returns else second, arrive[1]):
            inc(SY.dma_start(T.w1[:, a:b], T.lay[:, C + a:C + b]), nm, 16)

    chunk = C // 8
    inc(V.memset(T.zero[:], 0.0), "zs")
    wait(A, "zs")
    vz = 3 if returns else 2
    for c in range(vz, 8):
        inc(A.activation(T.sw[:, chunk * c:chunk * (c + 1)], T.zero[:], Copy), "zw")
    if returns:
        load_second()
        cnt["as"] = bits(topo.mask(cores[twin], core))
        wait(SY, "as")
    else:
        for a in range(2):
            inc(SY.dma_start(T.st[64 * a:64 * (a + 1), :], T.lay[14 + a:128:16, C:2 * C]), "ls", 16)
    early = 3 if returns else 1

    inc(g.iota(T.pi[:, 0:1], [[1, 1]], 0, 1), "gi")
    wait(V, "gi")
    inc(g.iota(T.dc[:], [[1, BW]], 0, 0, allow_small_or_imprecise_dtypes=True), "gj")
    inc(g.iota(T.dg[:], [[1, BW]], 0, -1, allow_small_or_imprecise_dtypes=True), "gi")
    col = {}

    def column(nm, src, s1, s2, o0, o1):
        col[nm] = (T.mb if nm == "diag" else T.mk)[:, len(col):len(col) + 1]
        inc(V.tensor_scalar(col[nm], src, s1, s2, o0, o1), "su")

    def band(o, src, at, weight):
        inc(V.tensor_scalar(o, src, at, weight, op.is_equal, op.mult), "su")

    p31, p32, p29, p2, p15 = [T.pm[:, k:k + 1] for k in range(5)]
    for o, m in ((p31, 31), (p32, 32), (p29, 29), (p2, 2), (p15, 15)):
        inc(V.tensor_scalar(o, T.pi[:, 0:1], m, None, op.bitwise_and), "su")
    column("shift", T.pi[:, 0:1], 64.0, float(SHIFT), op.is_lt, op.mult)
    wait(V, "su")
    column("row", p31, 4.0, 3.0, op.mult, op.add)
    column("xy", p32, 63.0 / 32, 1.0, op.mult, op.add)
    column("t1", p29, 4.0, 3.0, op.mult, op.add)
    column("h0", p2, 0.0, 1.0, op.is_equal, op.mult)
    column("h1", p2, 2.0, 1.0, op.is_equal, op.mult)
    column("h63", p15, 8.0, 63.0, op.is_ge, op.mult)
    column("slope", p15, 14.0, 1.0 / 128, op.is_ge, op.mult)
    column("diag", p15, 7.0, -105.0, op.mult, op.add)
    wait(V, "su")
    wait(V, "gj")
    band(T.mv[:, 2 * BW:3 * BW], T.dc[:], col["row"], col["xy"])
    wait(PE, "su")
    column("to", p32, 0.25, col["t1"], op.mult, op.add)
    column("wr", col["h63"], 1.0, 1.0, op.add, op.mult)
    column("ww", col["h63"], 1.0, -1.0 / 16, op.add, op.mult)
    column("down", p15, 8.0, -8.0, op.is_ge, op.mult)
    column("up", p15, 8.0, 8.0, op.is_lt, op.mult)
    inc(V.memset(T.kap[:], KAPPA), "su")
    wait(V, "gi")
    band(T.ib[:], T.dg[:, 0:128], 0.0, 1.0)
    wait(V, "lp")
    inc(V.tensor_scalar(T.lc[0:64, :], T.li[0:64, 0:4 * K], 1.0 / 16, 1055.5 + 1.0 / 32, op.mult, op.add), "sv")
    wait(V, "su")
    for h in range(2):
        band(T.mv[:, BW * h:BW * (h + 1)], T.dc[:], col["to"], col["h%d" % h])
    wait(V, "lq")
    inc(V.tensor_scalar(T.w0[:, C:CF], T.li[:, 4 * K:4 * K + 2], col["slope"], None, op.mult), "fz")
    wait(V, "ld")
    inc(V.tensor_scalar(T.lf[:], T.li[:, 0:4 * K], col["shift"], None, op.add), "sf")

    wins = (T.w0, T.w1, T.v0, T.v1, T.sw)
    ps = (T.ps0, T.ps1)
    ap = (T.ap0, T.ap1)
    place = {}
    free = [0]
    seen = {}

    def once(key):
        new = key not in seen
        seen[key] = 1
        return new

    def spread(bank, bt, rows, stop):
        for h in range(2):
            for j in range(4):
                mm = PE.matmul(bank[:, h:K:2], T.mv[0:rows, BW * h + 3 - j:BW * h + 131 - j],
                               T.lf[0:rows, K * j + KB * bt:K * j + KB * (bt + 1)], False, stop and h + j == 4)
        return mm

    def rounds(bt):
        wait(V, "mx%d" % bt)
        inc(V.tensor_scalar(T.rw[:, 2 * K * bt:2 * K * bt + K], ps[bt][:, 0:K], 1.0 / 16, 1023.5, op.mult, op.add),
            "rr%d" % bt)
        inc(V.tensor_scalar(T.rw[:, 2 * K * bt + K:2 * K * (bt + 1)], ps[bt][:, 0:K], ROUND1024, -ROUND1024,
                            op.add, op.add), "ww%d" % bt)

    def whole_place(o, bank, sem):
        inc(V.tensor_scalar(o, bank[:, 0:K], FLOOR, -FLOOR - 0.5, op.add, op.add), sem)

    def keep_place(bt, bank, sem):
        place[bt] = (free[0], place.get(bt, (None,))[0])
        whole_place(T.pos[:, free[0]:free[0] + K], bank, sem)
        free[0] += K

    def cells(bt):
        if once("cells"):
            wait(PE, "su")
            wait(PE, "dv0")
        if "dv%d" % (1 - bt) in cnt:
            wait(PE, "dv%d" % (1 - bt))
        for a, nm in enumerate(("rr", "ww")):
            wait(PE, nm + str(bt))
            c0 = 2 * K * bt + K * a
            for h in range(2):
                mm = PE.matmul(T.pso[:, 0:KB], T.mm[:, 128 * (2 * a + h):128 * (2 * a + h + 1)],
                               T.rw[:, c0 + h:c0 + K:2], a + h == 0, a + h == 2)
        inc(mm, "s2%d" % bt)

    def offsets(bt, o):
        wait(V, "s2%d" % bt)
        inc(V.tensor_scalar(o, T.pso[:, 0:KB], -65.0 * (1024 - SHIFT // 16), None, op.add), "dv%d" % bt)

    def make_bands(l0, w):
        for l in range(2):
            inc(V.tensor_scalar(T.band[:, BW * (l0 + l):BW * (l0 + l + 1)], T.dg[:], col["diag"], w[:, C + l:C + l + 1],
                                op.is_equal, op.mult), "ep")

    wait(PE, "sv")
    for j in range(4):
        mm = PE.matmul(T.pso[:, 0:K], T.mv[0:64, 2 * BW + 3 - j:2 * BW + 131 - j], T.lc[0:64, K * j:K * (j + 1)],
                       j == 0, j == 3)
    inc(mm, "sv")
    wait(V, "sv")
    inc(V.tensor_scalar(T.off[:, 0:K], T.pso[:, 0:K], -65.0 * 1056, None, op.add), "dv0")
    wait(PE, "su")
    wait(PE, "sf")
    wait(V, "fz")
    make_bands(0, T.w0)
    if not returns:
        inc(V.memset(T.sw[:, 0:chunk * vz], 0.0), "zw")
    for k, (d, w) in enumerate((("down", "wr"), ("up", "wr"), ("down", "ww"), ("up", "ww"))):
        band(T.mm[:, 128 * k:128 * (k + 1)], T.dg[:, 0:128], col[d], col[w])

    def place_slopes():
        wait(SY, "zw")
        for a in range(2):
            src = T.st[64 * a:64 * (a + 1), :] if returns else T.lay[14 + a:128:16, C:2 * C]
            inc(SY.dma_start(T.sw[14 + a:128:16, :], src), "lz", 16)
        SY.sem_inc(S.go, 1)

    if not returns:
        place_slopes()

    def send_piece(l, a, b, m):
        wait(g, "lw2" if b == LEAD else arrive[1][-1] if l and a else "lw%d" % l)
        if b > C:
            wait(g, "fz")
        if (l, a) == ((1, MID) if returns else (0, LEAD)):
            g.wait_ge(S.go, 1)
            if returns:
                wait(g, "half")
        remote(cores[twin], (T.v0, T.v1)[l][:, a:b], (T.w0, T.w1)[l][:, a:b], "av%d" % l, m,
               "half" if returns and (l, a) == (1, 0) else "sent")

    for x in pieces:
        if x[0] == 0 or returns:
            send_piece(*x)
    if not returns:
        wait(g, "ls")
        remote(cores[twin], T.st[:], T.st[:], "as", topo.mask(core, cores[twin]))

    if returns:
        own_banks = [(T.ao0, 0, H), (T.ao1, H, R)]
    else:
        own_banks = [(T.ao0, 0, H), (T.ao1, H, H + H // 2), (T.ao2, H + H // 2, R)]
    own_all = sum(len(w) for (o, s0, w) in phases if o == rank) + int(not returns)
    own_done = {0: 0, 1: 0}

    def own_add(bt, lhs, buf, c0):
        own_done[bt] += 1
        for j, (bank, a, b) in enumerate(own_banks):
            if a // H == bt:
                mm = PE.matmul(bank[:, 0:b - a], lhs, buf[:, c0 + a:c0 + b], own_done[bt] == 1, own_done[bt] == own_all)
                if own_done[bt] == own_all:
                    inc(mm, "f%d" % j)

    def late_gathers():
        for nm in arrive[early]:
            wait(A, nm)
        for bt in range(2):
            P0, o0 = early * R + bt * H, early * K + bt * KB
            inc(A.activation(T.p[:, P0:P0 + H], wins[early][:, 0:C].indirect(T.off[:, o0:o0 + KB]), Copy), "gl%d" % bt)
            wait(PE, "gl%d" % bt)
            own_add(bt, T.ib[:], T.p, early * R)

    def send_sum(j):
        a, b = parts[j]
        wait(g, "ev%d" % j)
        remote(partner, T.pin[:, a:b], T.po[:, a:b], "pa%d" % j, hop_mask)

    def run_phase(pk, base):
        owner, s0, wl = phases[pk]
        nh = 2 * len(wl)
        hops = s0 + len(wl) < STEPS

        def info(k):
            bt, j = k % 2, k // 2
            return bt, j, s0 + j, (base + j) * R + bt * H

        def moves(k):
            return 0 <= k < nh and info(k)[2] < STEPS - 1

        def landed(k):
            return k < 2 and pk > 0

        def share(k):
            if k == 0:
                return OPT["kvh"] if pk else OPT["kv0"]
            if not moves(k):
                return KB if returns else OPT["kvl"] if k % 2 else OPT["kv"]
            return OPT["kv"]

        def gather(q, k):
            bt, j, s, P0 = info(k)
            if landed(k):
                buf, o0, sem = T.mi, (2 * (pk - 1) + bt) * M, "am%d" % (2 * pk + bt)
            else:
                buf, o0, sem = T.off, (base + j) * K + bt * KB, "dv%d" % (bt if s else 0)
            ka = KB - share(k)
            if q is A and not ka:
                wait(A, "ac%d" % bt)
                inc(A.activation(T.se[:, H * bt:H * (bt + 1)], ap[bt][:], Copy), "eb%d" % bt)
                return
            wait(q, sem)
            w = 4 if pk == 0 and s == early else wl[j]
            if once((w, q is A)):
                for nm in arrive[w]:
                    wait(q, nm)
            win = wins[w][:, 0:C]
            if q is A:
                inc(A.activation(T.p[:, P0:P0 + 16 * ka], win.indirect(buf[:, o0:o0 + ka]), Copy), "ga%d" % bt)
            elif not ka:
                wait(V, "eb%d" % bt)
                for jp, (a, b) in enumerate(parts):
                    if a // H == bt:
                        c0 = o0 + (a - H * bt) // 16
                        inc(V.tensor_tensor(T.po[:, a:b], win.indirect(buf[:, c0:c0 + (b - a) // 16]), T.se[:, a:b],
                                            op.add), "ev%d" % jp)
                        send_sum(jp)
            else:
                if wl[j] == 2 and once("bands"):
                    make_bands(2, T.v0)
                if landed(k):
                    c0 = free[0]
                    free[0] += 2 * K
                    place[bt] = (c0, c0 + K)
                    inc(V.tensor_copy(T.pos[:, c0:c0 + 2 * K], buf[:, o0 + KB:o0 + M]), "cv%d" % bt)
                inc(V.tensor_copy(T.p[:, P0 + 16 * ka:P0 + H], win.indirect(buf[:, o0 + ka:o0 + KB])), "gd%d" % bt)

        def positions(k, stop):
            bt = k % 2
            if once("twice"):
                wait(PE, "su")
            a, b = place[bt]
            PE.matmul(ps[bt][:, 0:K], T.i2[:], T.pos[:, a:a + K], False, False)
            return PE.matmul(ps[bt][:, 0:K], T.im[:], T.pos[:, b:b + K], False, stop)

        def open_bank(k):
            bt = k % 2
            if "dx%d" % bt in cnt:
                wait(PE, "dx%d" % bt)
            PE.matmul(ps[bt][:, 0:K], T.ib[:], T.kap[:], True, False)
            if pk == 0 and k < 2:
                spread(ps[bt], bt, 128, False)
            elif not landed(k):
                positions(k, False)

        def slopes(k):
            bt, j, s, P0 = info(k)
            if once(("band", wl[j] // 2)):
                wait(PE, "ep")
            if landed(k):
                wait(PE, "cv%d" % bt)
                positions(k, False)
            wait(PE, "ga%d" % bt)
            wait(PE, "gd%d" % bt)
            b0 = BW * wl[j] + 7
            for i in range(8):
                mm = PE.matmul(ps[bt][:, 0:K], T.band[:, b0 - i:b0 - i + 128], T.p[:, P0 + i:P0 + H:8], False, i == 7)
            inc(mm, "mx%d" % bt)

        def new_place(k):
            bt, j, s, P0 = info(k)
            left = len(wl) - 1 - j
            m0 = (2 * pk + bt) * M + KB
            if s < STEPS - 2 and left:
                keep_place(bt, ps[bt], "dx%d" % bt)
            if hops and left < 2:
                whole_place(T.mo[:, m0 + K * left:m0 + K * (left + 1)], ps[bt], "dx%d" % bt)

        def sums(k):
            bt, j, s, P0 = info(k)
            if owner != rank:
                if moves(k):
                    last = j == len(wl) - 1 or s == STEPS - 2
                    mm = PE.matmul(ap[bt][:], T.ib[:], T.p[:, P0:P0 + H], j == 0, last)
                    if last:
                        inc(mm, "ac%d" % bt)
                return
            if s == early:
                return
            if not moves(k):
                wait(PE, "pa%d" % bt)
                own_add(bt, T.im[:], T.pin, 0)
                wait(PE, "ga%d" % bt)
                wait(PE, "gd%d" % bt)
            own_add(bt, T.ib[:], T.p, P0 - bt * H)

        def new_offsets(k):
            bt, j, s, P0 = info(k)
            m0 = (2 * pk + bt) * M
            o0 = (base + j + 1) * K + bt * KB
            if j < len(wl) - 1:
                offsets(bt, T.off[:, o0:o0 + KB])
                return
            offsets(bt, T.mo[:, m0:m0 + KB])
            wait(g, "dx%d" % bt)
            wait(g, "dv%d" % bt)
            remote(partner, T.mi[:, m0:m0 + M], T.mo[:, m0:m0 + M], "am%d" % (2 * pk + 2 + bt), hop_mask)
            if pk == 0 and bt == 1 and not returns:
                g.sem_inc(S.gw, 1)
                SY.wait_ge(S.gw, 1)
                load_second()
                for x in second:
                    send_piece(*x)

        open_bank(0)
        if pk == 0:
            open_bank(1)
            for bt in range(2):
                PE.matmul(ap[bt][:, 0:K], T.ib[:], T.kap[:], True, False)
                mm = spread(ap[bt], bt, 64, True)
            inc(mm, "sf")
        for k in range(nh + 2):
            if moves(k - 2):
                new_offsets(k - 2)
            ahead = k == 1 and pk == 0
            if k < nh:
                gather(A, k)
            if ahead:
                gather(V, k)
                wait(V, "sf")
                for bt in range(2):
                    keep_place(bt, ap[bt], "su")
                for buf, val in ((T.i2, 2.0), (T.im, -1.0)):
                    band(buf[:], T.dg[:, 0:128], 0.0, val)
            if pk == 0 and returns and 2 <= k <= vz + 1:
                inc(V.memset(T.sw[:, chunk * (k - 2):chunk * (k - 1)], 0.0), "zw")
                if k == vz + 1:
                    place_slopes()
            if moves(k - 1):
                rounds((k - 1) % 2)
            if k < nh and not ahead:
                gather(V, k)
            if moves(k - 1):
                new_place(k - 1)
                cells((k - 1) % 2)
            if moves(k):
                slopes(k)
            if k < nh:
                sums(k)
            if moves(k + 1) and (pk or k):
                open_bank(k + 1)
        if pk == 0 and once("bands"):
            wait(V, "av0")
            make_bands(2, T.v0)
        if pk == 1:
            late_gathers()
        if owner != rank and hops:
            for bt in range(2):
                wait(V, "ac%d" % bt)
                inc(V.tensor_scalar(T.po[:, H * bt:H * (bt + 1)], ap[bt][:], -1.0, None, op.mult), "ev%d" % bt)
                send_sum(bt)

    base = 0
    for pk in range(len(phases)):
        run_phase(pk, base)
        base += len(phases[pk][2])

    for j, (a, b) in enumerate(parts if returns else [x[1:] for x in own_banks]):
        st, sem = ((A, "sa"), (SY, "sb"))[j % 2]
        ev = "yy%d" % j
        if returns:
            bt = a // H
            wait(V, "f%d" % bt)
            wait(V, "pa%d" % j)
            inc(V.tensor_tensor(T.yo[:, a:b], own_banks[bt][0][:, a - H * bt:b - H * bt], T.pin[:, a:b], op.add), ev)
        elif st is A:
            wait(A, "f%d" % j)
            inc(A.activation(T.yo[:, a:b], own_banks[j][0][:, 0:b - a], Copy), ev)
        else:
            wait(V, "f%d" % j)
            inc(V.tensor_copy(T.yo[:, a:b], own_banks[j][0][:, 0:b - a]), ev)
        wait(st, ev)
        inc(st.dma_start(T.y[:, a:b], T.yo[:, a:b]), sem, 16)
    wait(g, "sent")
    wait(A, "sa")
    wait(SY, "sb")
